import numpy as np
import ml_dtypes


def mxq(x, axis, fmt="e4m3"):
    dtype, down = {"e4m3": (ml_dtypes.float8_e4m3fn, 7), "e5m2": (ml_dtypes.float8_e5m2, 14)}[fmt]
    v = np.moveaxis(np.asarray(x, np.float32).astype(ml_dtypes.bfloat16).astype(np.float64), axis, -1)
    blocks = v.reshape(v.shape[:-1] + (-1, 32))
    amax = np.abs(blocks).max(-1, keepdims=True)
    byte = np.maximum(np.where(amax > 0, np.frexp(amax)[1] - 1 + 127, 0) - down, 1)
    scale = np.exp2(byte - 127.0)
    codes = (blocks / scale).astype(np.float32).astype(dtype).astype(np.float64)
    return np.moveaxis((codes * scale).reshape(v.shape), -1, axis)


WIDE = False


def mx_kscale(k):
    if not WIDE:
        return np.ones(k)
    levels = np.array([10, -10, 5, -5, 0])
    if k % 512:
        return np.exp2(np.random.permutation(np.resize(levels, k // 32))).repeat(32)
    a = np.empty((k // 512, 16))
    for p in range(k // 512):
        a[p, :8] = np.random.permutation(np.resize(levels, 8))
        for g in range(8):
            far = levels[np.abs(levels - a[p, g]) >= 10]
            a[p, g + 8] = far[np.random.randint(len(far))]
    return np.exp2(a.ravel()).repeat(32)


def f64(x):
    return np.asarray(x).astype(np.float64)


def striped(idx):
    return np.tile(idx.reshape(-1, 16).T, (8, 1)).astype(np.uint16)


def unstriped(offs):
    return offs[:16].T.reshape(-1).astype(np.int64)


E2M1 = np.array([0.0, 0.5, 1.0, 1.5, 2.0, 3.0, 4.0, 6.0, -0.0, -0.5, -1.0, -1.5, -2.0, -3.0, -4.0, -6.0])


def pack_weight(w, fmt):
    k, n = w.shape
    w = f64(np.asarray(w, np.float32).astype(ml_dtypes.bfloat16)).reshape(k // 32, 32, n)
    amax = np.abs(w).max(1)
    if fmt == "e4m3":
        byte = np.frexp(amax)[1] - 1 + 127 - 7
    else:
        mant, ex = np.frexp(amax / 6.0)
        byte = np.where(mant > 0.5, ex, ex - 1) + 127
    byte = np.clip(np.where(amax > 0, byte, 1), 1, 254)
    scaled = (w * np.exp2(127.0 - byte)[:, None, :]).reshape(k, n).astype(np.float32)
    by_word = np.ascontiguousarray(scaled.reshape(k // 512, 128, 4, n).transpose(0, 1, 3, 2))
    if fmt == "e4m3":
        words = by_word.astype(ml_dtypes.float8_e4m3fn).view(np.uint8)
    else:
        c = by_word.astype(ml_dtypes.float4_e2m1fn).view(np.uint8) & 0xF
        words = (c[..., 0::2] | (c[..., 1::2] << 4)).reshape(k // 512, 128, 2 * n)
    return np.ascontiguousarray(words), np.ascontiguousarray(byte.astype(np.uint8).reshape(k // 512, 16, n))


def unpack_weight(words, scales, fmt):
    g, _, n = scales.shape
    words = np.ascontiguousarray(words).reshape(g, 128, n, -1)
    if fmt == "e4m3":
        vals = words.view(ml_dtypes.float8_e4m3fn).astype(np.float64)
    else:
        nib = np.empty((g, 128, n, 4), np.uint8)
        nib[..., 0::2] = words & 0xF
        nib[..., 1::2] = words >> 4
        vals = E2M1[nib]
    vals = vals * np.repeat(np.exp2(scales.astype(np.float64) - 127.0), 8, axis=1)[..., None]
    return vals.transpose(0, 1, 3, 2).reshape(g * 512, n)


def gelu(v):
    return 0.5 * v * (1.0 + np.tanh(np.sqrt(2.0 / np.pi) * (v + 0.044715 * v**3)))


def bf(x):
    return np.asarray(x, np.float32).astype(ml_dtypes.bfloat16)


def planes(Y):
    n, m = Y.shape
    b = f64(bf(Y)).reshape(n // 32, 32, m)
    amax = np.abs(b).max(1)
    byte = np.clip(np.where(amax > 0, np.frexp(amax)[1] - 1 + 127 - 7, 1), 1, 254)
    codes = (b * np.exp2(127.0 - byte)[:, None, :]).reshape(n, m).astype(np.float32).astype(ml_dtypes.float8_e4m3fn).view(np.uint8)
    words = codes.reshape(n // 512, 128, 4, m).transpose(0, 1, 3, 2)
    return np.ascontiguousarray(words), np.ascontiguousarray(byte.astype(np.uint8).reshape(n // 512, 16, m))


K, H, T, S, T2, P = 1024, 1024, 2048, 512, 2048, 512

def setup_inputs():
    n = np.random.standard_normal
    s, u = mx_kscale(K)[:, None], mx_kscale(H)[:, None]
    ys = np.exp(0.8 * n(H))
    perm = np.random.permutation(T2)
    d = {}
    d["tab_words"], d["tab_scales"] = pack_weight(n((K, T)) * s, "e4m3")
    d["tab2_words"], d["tab2_scales"] = pack_weight(0.8 * n((K, T)) * s, "e4m3")
    d["w1"] = (1.5 * n((K, H)) / K ** 0.5 / s).astype(np.float32)
    d["g1"] = (1.2 * np.exp(0.3 * n(H)) * u[:, 0]).astype(np.float32)
    d["w2"] = (0.8 * n((K, H)) / K ** 0.5 / s * u.T).astype(np.float32)
    d["w3_words"], d["w3_scales"] = pack_weight((0.3 * n((K, H)) / K ** 0.5 - np.eye(K, H)) / s * u.T, "e2m1")
    d["wg1"] = np.exp(0.3 * n((128, S))).astype(np.float32)
    d["wg2"] = np.exp(0.3 * n((128, S))).astype(np.float32)
    d["page0"] = (n((H, T2)) * u).astype(np.float32)
    d["mset"] = (0.7 * n((H, P)) * u).astype(np.float32)
    d["w4_words"], d["w4_scales"] = pack_weight(0.4 * n((H, H)) / H ** 0.5 / u, "e4m3")
    d["w5"] = (n((H, H)) / H ** 0.5 / u * ys).astype(np.float32)
    d["g2"] = (0.8 * np.exp(0.2 * n(H)) * ys / u[:, 0]).astype(np.float32)
    d["offs"] = striped(np.random.permutation(T)[:S])
    d["offs2"] = striped(np.random.permutation(T)[:S])
    d["offs3"] = striped(perm[:S])
    d["offs4"] = striped(perm[S:2 * S])
    d["offs5"] = striped(np.random.permutation(T2)[:P])
    return d

def reference(tab_words, tab_scales, tab2_words, tab2_scales, w1, g1, w2, w3_words, w3_scales, wg1, wg2, page0, mset, w4_words, w4_scales, w5, g2, offs, offs2, offs3, offs4, offs5):
    v = unpack_weight(tab_words, tab_scales, "e4m3")[:, unstriped(offs)]
    v2 = unpack_weight(tab2_words, tab2_scales, "e4m3")[:, unstriped(offs2)]
    h1 = f64(g1)[:, None] * np.tanh(mxq(f64(w1), 0, "e4m3").T @ v)
    h2 = mxq(f64(w2), 0, "e4m3").T @ v2 + unpack_weight(w3_words, w3_scales, "e2m1").T @ v2
    page = f64(page0).copy()
    page[:, unstriped(offs3)] = np.tile(f64(wg1), (H // 128, 1)) * h1
    page[:, unstriped(offs4)] = np.tile(f64(wg2), (H // 128, 1)) * h2
    x = page[:, unstriped(offs5)]
    z = mxq(x + f64(mset), 0, "e4m3")
    e = np.cos(unpack_weight(w4_words, w4_scales, "e4m3").T @ z)
    y = e * ((mxq(f64(w5), 0, "e4m3").T @ z) + f64(g2)[:, None] * x)
    words, scales = planes(y)
    return y, words, scales

@@ -1,0 +1,380 @@
+import math
+from contextlib import ExitStack
+
+import concourse.mybir as mybir
+from concourse.masks import make_identity
+
+K, H, T, S, T2, M = 1024, 1024, 2048, 512, 2048, 512
+FLOPS = 5 * 2 * K * H * S
+
+F32 = mybir.dt.float32
+BF16 = mybir.dt.bfloat16
+I32 = mybir.dt.int32
+U32 = mybir.dt.uint32
+U16 = mybir.dt.uint16
+U8 = mybir.dt.uint8
+FP8X4 = mybir.dt.float8_e4m3fn_x4
+FP4X4 = mybir.dt.float4_e2m1fn_x4
+ALU = mybir.AluOpType
+ACT = mybir.ActivationFunctionType
+
+P = 128
+PACK = 4
+K_PASS = P * PACK
+PASSES = 2
+SLICES = H // P
+CHUNK = 256
+QUADS = 4
+TWO_PI = 2.0 * math.pi
+
+
+def tile_list_churn_overrun_slots_kernel(
+    tc, tab_words, tab_scales, tab2_words, tab2_scales, w1, g1, w2, w3_words, w3_scales, wg1, wg2, page0, mset,
+    w4_words, w4_scales, w5, g2, offs, offs2, offs3, offs4, offs5, out_0, out_1, out_2,
+):
+    nc = tc.nc
+    with ExitStack() as ctx:
+        keep = ctx.enter_context(tc.tile_pool(name="keep", bufs=1))
+        ring = ctx.enter_context(tc.tile_pool(name="ring", bufs=1))
+        psum = ctx.enter_context(tc.psum_pool(name="psum", bufs=1))
+
+        def load_list(dram, name):
+            t = keep.tile([P, S // 16], U16, name=name)
+            nc.sync.dma_start(t[:], dram)
+            return t
+
+        def row_tile(tag, bufs, dtype=F32):
+            return ring.tile([P, M], dtype, name=tag, tag=tag, bufs=bufs, align_bytes=64)
+
+        def stage_tile():
+            return ring.tile([P, 2048], BF16, name="stage", tag="stage", bufs=6, align_bytes=64)
+
+        def raw_tile(dtype=F32):
+            return ring.tile([P, PACK, CHUNK], dtype, name="raw", tag="raw", bufs=4, align_bytes=64)
+
+        def big_tile(tag, shape, dtype, bufs=1):
+            return ring.tile(shape, dtype, name=tag, tag=tag, bufs=bufs, align_bytes=64)
+
+        def acc_bank():
+            return psum.tile([P, M], F32, name="acc", tag="acc", bufs=4)
+
+        def turn_bank():
+            return psum.tile([P, M], F32, name="turn", tag="turn", bufs=4)
+
+        tab_sc = keep.tile([P, T], U8, name="tab_sc", align_bytes=64)
+        tab2_sc = keep.tile([P, PASSES, T], U8, name="tab2_sc", align_bytes=64)
+        w3_sc = keep.tile([P, PASSES, H], U8, name="w3_sc", align_bytes=64)
+        w4_sc = keep.tile([P, H], U8, name="w4_sc", align_bytes=64)
+        g1_sb = keep.tile([P, SLICES], F32, name="g1_sb")
+        g2_sb = keep.tile([P, PASSES, PACK], F32, name="g2_sb")
+        ident = keep.tile([P, P], F32, name="ident")
+        nc.gpsimd.memset(tab_sc[:].bitcast(I32), 0)
+        nc.vector.memset(tab2_sc[:].bitcast(I32), 0)
+        nc.vector.memset(w3_sc[:].bitcast(I32), 0)
+        nc.vector.memset(w4_sc[:].bitcast(I32), 0)
+
+        def load_packed_scales(queue, dst, dram):
+            for q in range(QUADS):
+                queue.dma_start(dst[32 * q : 32 * q + 8, :].bitcast(I32), dram[:, 4 * q : 4 * q + 4, :].bitcast(I32))
+
+        def load_plane_scales(dst, dram):
+            for q in range(QUADS):
+                nc.sync.dma_start(
+                    dst[32 * q : 32 * q + 4, :, :].bitcast(I32),
+                    dram[:, 4 * q : 4 * q + 4, :].rearrange("a r c -> r a c").bitcast(I32),
+                )
+
+        with nc.allow_non_contiguous_dma(reason="one gain a partition"):
+            nc.gpsimd.dma_start(g1_sb[:], g1.rearrange("(s p) -> p s", p=P))
+        make_identity(nc, ident[:])
+        nc.gpsimd.dma_start(g2_sb[:], g2.rearrange("(g p t) -> p g t", p=P, t=PACK))
+
+        def load_table(dram, a, tag, bufs):
+            t = big_tile(tag, [P, T], I32, bufs=bufs)
+            nc.sync.dma_start(t[:], dram[a].rearrange("p t i -> p (t i)").bitcast(I32))
+            return t
+
+        def gather_words(table, lst, name):
+            t = keep.tile([P, S], U32, name=name, align_bytes=64)
+            nc.vector.tensor_copy(t[:], table[:].bitcast(U32).indirect(lst[:]))
+            return t
+
+        def gather_scales(window, lst, name):
+            t = keep.tile([P, S], U8, name=name, align_bytes=64)
+            nc.vector.tensor_copy(t[:], window.indirect(lst[:]))
+            return t
+
+        def load_raw(w, a, c0):
+            raw = raw_tile()
+            rows = w[a * K_PASS : (a + 1) * K_PASS, c0 : c0 + CHUNK]
+            nc.sync.dma_start(raw[:], rows.rearrange("(p j) c -> p j c", j=PACK))
+            return raw
+
+        def weight_chunk(w, c, raws=None):
+            stage = stage_tile()
+            for a in range(PASSES):
+                raw = raws[a] if raws else load_raw(w, a, c * CHUNK)
+                dst = stage[:, a * 1024 : (a + 1) * 1024].rearrange("p (c i j) -> p c j i", i=4, j=PACK)
+                nc.scalar.copy(dst, raw[:].rearrange("p j (c i) -> p c j i", i=4))
+            codes = ring.tile([P, PASSES * CHUNK], U32, name="wcodes", tag="wcodes", bufs=4, align_bytes=64)
+            scales = ring.tile([P, PASSES * CHUNK], U8, name="wscales", tag="wscales", bufs=4, align_bytes=64)
+            nc.vector.quantize_mx(out=codes[:].bitcast(FP8X4), scales=scales[:], in_=stage[:])
+            return codes, scales
+
+        def load_page(s):
+            page = big_tile("page%d" % s, [P, T2], F32)
+            nc.sync.dma_start(page[:], page0[s * P : (s + 1) * P, :])
+            return page
+
+        def load_mset(s):
+            t = row_tile("mset", 3)
+            nc.sync.dma_start(t[:], mset[s * P : (s + 1) * P, :])
+            return t
+
+        def chunk_cols(a, s):
+            c0 = a * CHUNK + (s % 2) * P
+            return slice(c0, c0 + P)
+
+        def put_h1(s, wq, page):
+            codes, scales = wq
+            acc = acc_bank()
+            for a in range(PASSES):
+                cols = chunk_cols(a, s)
+                nc.tensor.matmul_mx(
+                    out=acc[:], lhsT=codes[:, cols].bitcast(FP8X4), lhsT_scale=scales[:, cols],
+                    rhs=v_words[a][:].bitcast(FP8X4), rhs_scale=v_scales[4 * a : P, :],
+                    start=(a == 0), stop=(a == PASSES - 1),
+                )
+            gain = row_tile("gain", 8)
+            nc.scalar.activation(gain[:], wg1_sb[:], ACT.Copy, scale=g1_sb[:, s : s + 1])
+            h = row_tile("h", 6)
+            nc.scalar.activation(h[:], acc[:], ACT.Tanh)
+            nc.vector.tensor_tensor(page[:].indirect(lst3[:]), h[:], gain[:], ALU.mult)
+
+        def put_h2(s, wq, page):
+            codes, scales = wq
+            acc = acc_bank()
+            for a in range(PASSES):
+                cols = chunk_cols(a, s)
+                nc.tensor.matmul_mx(
+                    out=acc[:], lhsT=codes[:, cols].bitcast(FP8X4), lhsT_scale=scales[:, cols],
+                    rhs=v2_words[a][:].bitcast(FP8X4), rhs_scale=v2_scales[a][:],
+                    start=(a == 0), stop=False,
+                )
+            for a in range(PASSES):
+                nc.tensor.matmul_mx(
+                    out=acc[:], lhsT=w3_sb[:, a, 2 * s * P : 2 * (s + 1) * P].bitcast(FP4X4),
+                    lhsT_scale=w3_sc[:, a, s * P : (s + 1) * P],
+                    rhs=v2_words[a][:].bitcast(FP8X4), rhs_scale=v2_scales[a][:],
+                    start=False, stop=(a == PASSES - 1),
+                )
+            h = row_tile("h", 6)
+            nc.scalar.copy(h[:], acc[:])
+            nc.vector.tensor_tensor(page[:].indirect(lst4[:]), h[:], wg2_sb[:], ALU.mult)
+
+        x_dealt = {}
+        sums = {}
+        z_turned = {}
+        z_codes = {}
+        z_scales = {}
+
+        def read_page(s, page, ms):
+            a, q = divmod(s, QUADS)
+            x = row_tile("x", 3)
+            nc.vector.tensor_copy(x[:], page[:].indirect(lst5[:]))
+            if q == 0:
+                x_dealt[a] = big_tile("table", [P, PACK, M], F32, bufs=2)
+                z_turned[a] = keep.tile([P, 4, 2, P, 2], BF16, name="z_turned%d" % a, align_bytes=64)
+            queue = nc.sync if s >= SLICES - 2 else nc.gpsimd
+            for t in range(PACK):
+                queue.dma_start(x_dealt[a][32 * q : 32 * q + 32, t, :], x[t:P:PACK, :])
+            bank = turn_bank()
+            for i, src in enumerate((ms, x)):
+                for c in range(4):
+                    nc.tensor.matmul(
+                        bank[:, c * P : (c + 1) * P], src[:, c * P : (c + 1) * P], ident[:],
+                        start=(i == 0 and c == 0), stop=(i == 1 and c == 3), is_transpose=True,
+                    )
+            sums[s] = bank
+
+        def empty_sum(s):
+            a, q = divmod(s, QUADS)
+            nc.scalar.copy(
+                z_turned[a][:, :, :, 32 * q : 32 * q + 32, :],
+                sums[s][:].rearrange("p (c q u e) -> p c u q e", c=4, u=2, e=2),
+            )
+
+        def quantise_z(a):
+            words = z_turned[a][:].rearrange("p c u q e -> p (c u q e)").bitcast(F32)
+            stage = stage_tile()
+            stage_words = stage[:].bitcast(F32)
+            for half in range(2):
+                bank = turn_bank()
+                for cc in range(2):
+                    for u in range(2):
+                        w0 = ((2 * half + cc) * 2 + u) * P
+                        o0 = u * 256 + cc * P
+                        nc.tensor.transpose(bank[:, o0 : o0 + P], words[:, w0 : w0 + P], ident[:])
+                dst = stage_words[:, half * 512 : (half + 1) * 512].rearrange("p (m u) -> p m u", u=2)
+                src = bank[:].rearrange("p (u m) -> p m u", u=2)
+                if a == PASSES - 1 and half == 1:
+                    nc.vector.tensor_copy(dst, src)
+                else:
+                    nc.scalar.copy(dst, src)
+            z_codes[a] = keep.tile([P, M], U32, name="z_codes%d" % a, align_bytes=64)
+            z_scales[a] = keep.tile([P, M], U8, name="z_scales%d" % a, align_bytes=64)
+            nc.vector.quantize_mx(out=z_codes[a][:].bitcast(FP8X4), scales=z_scales[a][:], in_=stage[:])
+
+        w5_stage = {}
+
+        def stage_w5(a, g):
+            stage = stage_tile()
+            view = stage[:].rearrange("p (t m j) -> p m j t", t=PACK, j=PACK)
+            for hh in range(2):
+                raw = load_raw(w5, a, g * K_PASS + hh * CHUNK)
+                nc.scalar.copy(view[:, 64 * hh : 64 * (hh + 1), :, :], raw[:].rearrange("p j (m t) -> p m j t", t=PACK))
+            w5_stage[(a, g)] = stage
+
+        w4_raw = {}
+
+        def load_w4(g):
+            raw = keep.tile([P, PASSES, K_PASS], I32, name="w4_raw%d" % g, align_bytes=64)
+            src = w4_words[:, :, g * K_PASS : (g + 1) * K_PASS, :].rearrange("a p c i -> p a (c i)").bitcast(I32)
+            nc.sync.dma_start(raw[:], src)
+            w4_raw[g] = raw
+
+        first_raw = [load_raw(w1, 0, 0)]
+        lst1 = load_list(offs, "lst1")
+        load_packed_scales(nc.sync, tab_sc, tab_scales)
+        first_raw.append(load_raw(w1, 1, 0))
+        wq1 = {0: weight_chunk(w1, 0, first_raw)}
+        wg1_sb = keep.tile([P, S], F32, name="wg1_sb")
+        v_scales = gather_scales(tab_sc[:], lst1, "v_scales")
+        v_words = {}
+        v_words[0] = gather_words(load_table(tab_words, 0, "table", 2), lst1, "v_words0")
+        nc.sync.dma_start(wg1_sb[:], wg1)
+        v_words[1] = gather_words(load_table(tab_words, 1, "table", 2), lst1, "v_words1")
+        lst3 = load_list(offs3, "lst3")
+        pages = {}
+        for s in range(2):
+            pages[s] = load_page(s)
+            put_h1(s, wq1[0], pages[s])
+        load_plane_scales(tab2_sc, tab2_scales)
+        table2 = load_table(tab2_words, 0, "page6", 1)
+        wq2 = {0: weight_chunk(w2, 0)}
+        lst2 = load_list(offs2, "lst2")
+        v2_scales = [gather_scales(tab2_sc[:, a, :], lst2, "v2_scales%d" % a) for a in range(PASSES)]
+        v2_words = {}
+        v2_words[0] = gather_words(table2, lst2, "v2_words0")
+        v2_words[1] = gather_words(load_table(tab2_words, 1, "page7", 1), lst2, "v2_words1")
+        load_plane_scales(w3_sc, w3_scales)
+        w3_sb = keep.tile([P, PASSES, 2 * H], U8, name="w3_sb", align_bytes=64)
+        nc.sync.dma_start(w3_sb[:].bitcast(I32), w3_words.rearrange("a p c -> p a c").bitcast(I32))
+        wg2_sb = big_tile("wg2", [P, S], F32)
+        nc.sync.dma_start(wg2_sb[:], wg2)
+        lst4 = load_list(offs4, "lst4")
+        lst5 = load_list(offs5, "lst5")
+        wq1[1] = weight_chunk(w1, 1)
+        put_h2(0, wq2[0], pages[0])
+        read_page(0, pages[0], load_mset(0))
+        wq2[1] = weight_chunk(w2, 1)
+        put_h2(1, wq2[0], pages[1])
+        read_page(1, pages[1], load_mset(1))
+
+        for s in range(2, SLICES):
+            pages[s] = load_page(s)
+            ms = load_mset(s)
+            ahead = s // 2 + 1
+            if ahead < SLICES // 2:
+                if s % 2 == 0:
+                    wq1[ahead] = weight_chunk(w1, ahead)
+                else:
+                    wq2[ahead] = weight_chunk(w2, ahead)
+            if s >= 4:
+                stage_w5(s % 2, (s - 4) // 2)
+            if s >= 6:
+                load_w4(s - 6)
+            if s == 7:
+                load_packed_scales(nc.sync, w4_sc, w4_scales)
+            put_h1(s, wq1[s // 2], pages[s])
+            put_h2(s, wq2[s // 2], pages[s])
+            read_page(s, pages[s], ms)
+            empty_sum(s - 2)
+            if s == SLICES - 2:
+                quantise_z(0)
+        empty_sum(SLICES - 2)
+        empty_sum(SLICES - 1)
+        quantise_z(1)
+
+        w4_codes = big_tile("wg2", [P, PASSES, H], I32)
+        w4_scd = keep.tile([P, H], U8, name="w4_scd", align_bytes=64)
+        w5_codes = big_tile("page%d" % (SLICES - 1), [P, PASSES, H], U32)
+        w5_scales = keep.tile([P, PASSES, H], U8, name="w5_scales", align_bytes=64)
+        nc.vector.tensor_copy(
+            w4_scd[:].rearrange("p (g t b i) -> p g b t i", g=2, t=PACK, i=16),
+            w4_sc[:].rearrange("p (g b i t) -> p g b t i", g=2, t=PACK, i=16),
+        )
+        for g in range(2):
+            cols = slice(g * K_PASS, (g + 1) * K_PASS)
+            nc.vector.tensor_copy(
+                w4_codes[:, :, cols].rearrange("p a (t b i) -> p a b t i", t=PACK, i=4),
+                w4_raw[g][:].rearrange("p a (b i t) -> p a b t i", t=PACK, i=4),
+            )
+            for a in range(PASSES):
+                nc.vector.quantize_mx(
+                    out=w5_codes[:, a, cols].bitcast(FP8X4), scales=w5_scales[:, a, cols], in_=w5_stage[(a, g)][:]
+                )
+
+        out_rows = out_0.rearrange("(g p t) m -> g t p m", p=P, t=PACK)
+        banks_made = []
+
+        def second_product(codes, scale_of, cols):
+            i = len(banks_made)
+            late = i % 8 >= 4
+            bank = turn_bank() if late else acc_bank()
+            banks_made.append(bank)
+            order = (1, 0) if late else (0, 1)
+            for n, a in enumerate(order):
+                nc.tensor.matmul_mx(
+                    out=bank[:], lhsT=codes[:, a, cols].bitcast(FP8X4), lhsT_scale=scale_of(a, cols),
+                    rhs=z_codes[a][:].bitcast(FP8X4), rhs_scale=z_scales[a][:], start=(n == 0), stop=(n == 1),
+                )
+            return bank
+
+        for g in range(2):
+            y = big_tile("page%d" % g, [P, PACK, M], F32)
+            for t in range(PACK):
+                cols = slice(g * K_PASS + t * P, g * K_PASS + (t + 1) * P)
+                angle = second_product(w4_codes, lambda a, cc: w4_scd[4 * a : P, cc], cols)
+                lin = second_product(w5_codes, lambda a, cc: w5_scales[:, a, cc], cols)
+                turns = row_tile("gain", 8, I32)
+                nc.vector.tensor_scalar(turns[:], angle[:], 1.0 / TWO_PI, 0.25, ALU.mult, ALU.add)
+                total = row_tile("h", 6)
+                nc.vector.scalar_tensor_tensor(
+                    total[:], x_dealt[g][:, t, :], g2_sb[:, g, t : t + 1], lin[:], ALU.mult, ALU.add
+                )
+                rest = row_tile("mset", 3)
+                nc.vector.scalar_tensor_tensor(rest[:], turns[:], -TWO_PI, angle[:], ALU.mult, ALU.add)
+                e = row_tile("x", 3)
+                nc.scalar.activation(e[:], rest[:], ACT.Sin, bias=math.pi / 2)
+                engine = nc.vector if (g, t) == (1, PACK - 1) else nc.gpsimd
+                engine.tensor_tensor(y[:, t, :], e[:], total[:], ALU.mult)
+                nc.sync.dma_start(out_rows[g, t], y[:, t, :])
+            stage = stage_tile()
+            y_codes = keep.tile([P, M], U32, name="y_codes%d" % g, align_bytes=64)
+            y_scales = keep.tile([P, M], U8, name="y_scales%d" % g, align_bytes=64)
+            words_out = out_1[g].rearrange("p m t -> p (m t)").bitcast(I32)
+            for half in range(2):
+                ms = slice(half * 256, (half + 1) * 256)
+                src = y[:, :, ms].rearrange("p t (c i) -> p c t i", i=4)
+                part = stage[:, half * 1024 : (half + 1) * 1024]
+                dst = part.rearrange("p (c i t) -> p c t i", i=4, t=PACK)
+                if g == 1 and half == 0:
+                    nc.vector.tensor_copy(dst, src)
+                else:
+                    nc.scalar.copy(dst, src)
+                nc.vector.quantize_mx(out=y_codes[:, ms].bitcast(FP8X4), scales=y_scales[:, ms], in_=part)
+                nc.sync.dma_start(words_out[:, ms], y_codes[:, ms].bitcast(I32))
+            for q in range(QUADS):
+                queue = nc.scalar if (g == 1 and q % 2 == 1) else nc.sync
+                queue.dma_start(out_2[g, 4 * q : 4 * q + 4, :].bitcast(I32), y_scales[32 * q : 32 * q + 4, :].bitcast(I32))

@@ -50,7 +50,7 @@ def tile_list_churn_overrun_slots_kernel(
             return ring.tile([P, 2048], BF16, name="stage", tag="stage", bufs=6, align_bytes=64)
 
         def raw_tile(dtype=F32):
-            return ring.tile([P, PACK, CHUNK], dtype, name="raw", tag="raw", bufs=4, align_bytes=64)
+            return ring.tile([P, PACK, CHUNK], dtype, name="raw", tag="raw", bufs=7, align_bytes=64)
 
         def big_tile(tag, shape, dtype, bufs=1):
             return ring.tile(shape, dtype, name=tag, tag=tag, bufs=bufs, align_bytes=64)
@@ -87,7 +87,6 @@ def tile_list_churn_overrun_slots_kernel(
         with nc.allow_non_contiguous_dma(reason="one gain a partition"):
             nc.gpsimd.dma_start(g1_sb[:], g1.rearrange("(s p) -> p s", p=P))
         make_identity(nc, ident[:])
-        nc.gpsimd.dma_start(g2_sb[:], g2.rearrange("(g p t) -> p g t", p=P, t=PACK))
 
         def load_table(dram, a, tag, bufs):
             t = big_tile(tag, [P, T], I32, bufs=bufs)
@@ -122,12 +121,12 @@ def tile_list_churn_overrun_slots_kernel(
             return codes, scales
 
         def load_page(s):
-            page = big_tile("page%d" % s, [P, T2], F32)
+            page = big_tile("page", [P, T2], F32, bufs=7)
             nc.sync.dma_start(page[:], page0[s * P : (s + 1) * P, :])
-            return page
+            pages[s] = page
 
         def load_mset(s):
-            t = row_tile("mset", 3)
+            t = row_tile("mset", 5)
             nc.sync.dma_start(t[:], mset[s * P : (s + 1) * P, :])
             return t
 
@@ -135,8 +134,9 @@ def tile_list_churn_overrun_slots_kernel(
             c0 = a * CHUNK + (s % 2) * P
             return slice(c0, c0 + P)
 
-        def put_h1(s, wq, page):
-            codes, scales = wq
+        def put_h1(s):
+            codes, scales = wq1[s // 2]
+            page = pages[s]
             acc = acc_bank()
             for a in range(PASSES):
                 cols = chunk_cols(a, s)
@@ -145,14 +145,15 @@ def tile_list_churn_overrun_slots_kernel(
                     rhs=v_words[a][:].bitcast(FP8X4), rhs_scale=v_scales[4 * a : P, :],
                     start=(a == 0), stop=(a == PASSES - 1),
                 )
-            gain = row_tile("gain", 8)
+            gain = row_tile("gain_last", 1) if s == SLICES - 1 else row_tile("gain", 7)
             nc.scalar.activation(gain[:], wg1_sb[:], ACT.Copy, scale=g1_sb[:, s : s + 1])
             h = row_tile("h", 6)
             nc.scalar.activation(h[:], acc[:], ACT.Tanh)
             nc.vector.tensor_tensor(page[:].indirect(lst3[:]), h[:], gain[:], ALU.mult)
 
-        def put_h2(s, wq, page):
-            codes, scales = wq
+        def put_h2(s):
+            codes, scales = wq2[s // 2]
+            page = pages[s]
             acc = acc_bank()
             for a in range(PASSES):
                 cols = chunk_cols(a, s)
@@ -168,40 +169,45 @@ def tile_list_churn_overrun_slots_kernel(
                     rhs=v2_words[a][:].bitcast(FP8X4), rhs_scale=v2_scales[a][:],
                     start=False, stop=(a == PASSES - 1),
                 )
-            h = row_tile("h", 6)
+            h = row_tile("h_last", 1) if s == SLICES - 1 else row_tile("h", 6)
             nc.scalar.copy(h[:], acc[:])
             nc.vector.tensor_tensor(page[:].indirect(lst4[:]), h[:], wg2_sb[:], ALU.mult)
 
         x_dealt = {}
-        sums = {}
+        picked = {}
+        pages = {}
         z_turned = {}
         z_codes = {}
         z_scales = {}
 
-        def read_page(s, page, ms):
+        def read_page(s):
             a, q = divmod(s, QUADS)
-            x = row_tile("x", 3)
-            nc.vector.tensor_copy(x[:], page[:].indirect(lst5[:]))
+            x = row_tile("x", 6)
+            picked[s] = x
+            nc.vector.tensor_copy(x[:], pages[s][:].indirect(lst5[:]))
             if q == 0:
-                x_dealt[a] = big_tile("table", [P, PACK, M], F32, bufs=2)
                 z_turned[a] = keep.tile([P, 4, 2, P, 2], BF16, name="z_turned%d" % a, align_bytes=64)
-            queue = nc.sync if s >= SLICES - 2 else nc.gpsimd
-            for t in range(PACK):
-                queue.dma_start(x_dealt[a][32 * q : 32 * q + 32, t, :], x[t:P:PACK, :])
+            queue = nc.sync if s == SLICES - 1 else nc.gpsimd
+            queue.dma_start(out_0[s * P : (s + 1) * P, :], x[:])
+
+        def deal_x(g):
+            x_dealt[g] = big_tile("page", [P, PACK, M], F32, bufs=7)
+            rows = out_0[g * K_PASS : (g + 1) * K_PASS, :]
+            nc.sync.dma_start(x_dealt[g][:], rows.rearrange("(p t) m -> p t m", t=PACK))
+
+        def add_mset(s):
+            ms = load_mset(s)
             bank = turn_bank()
-            for i, src in enumerate((ms, x)):
+            for i, src in enumerate((ms, picked[s])):
                 for c in range(4):
                     nc.tensor.matmul(
                         bank[:, c * P : (c + 1) * P], src[:, c * P : (c + 1) * P], ident[:],
                         start=(i == 0 and c == 0), stop=(i == 1 and c == 3), is_transpose=True,
                     )
-            sums[s] = bank
-
-        def empty_sum(s):
             a, q = divmod(s, QUADS)
             nc.scalar.copy(
                 z_turned[a][:, :, :, 32 * q : 32 * q + 32, :],
-                sums[s][:].rearrange("p (c q u e) -> p c u q e", c=4, u=2, e=2),
+                bank[:].rearrange("p (c q u e) -> p c u q e", c=4, u=2, e=2),
             )
 
         def quantise_z(a):
@@ -221,7 +227,7 @@ def tile_list_churn_overrun_slots_kernel(
                     nc.vector.tensor_copy(dst, src)
                 else:
                     nc.scalar.copy(dst, src)
-            z_codes[a] = keep.tile([P, M], U32, name="z_codes%d" % a, align_bytes=64)
+            z_codes[a] = row_tile("gain_last" if a == 0 else "z_codes", 1, U32)
             z_scales[a] = keep.tile([P, M], U8, name="z_scales%d" % a, align_bytes=64)
             nc.vector.quantize_mx(out=z_codes[a][:].bitcast(FP8X4), scales=z_scales[a][:], in_=stage[:])
 
@@ -250,65 +256,76 @@ def tile_list_churn_overrun_slots_kernel(
         wq1 = {0: weight_chunk(w1, 0, first_raw)}
         wg1_sb = keep.tile([P, S], F32, name="wg1_sb")
         v_scales = gather_scales(tab_sc[:], lst1, "v_scales")
-        v_words = {}
-        v_words[0] = gather_words(load_table(tab_words, 0, "table", 2), lst1, "v_words0")
+        v_words = [gather_words(load_table(tab_words, a, "page", 7), lst1, "v_words%d" % a) for a in range(PASSES)]
         nc.sync.dma_start(wg1_sb[:], wg1)
-        v_words[1] = gather_words(load_table(tab_words, 1, "table", 2), lst1, "v_words1")
         lst3 = load_list(offs3, "lst3")
-        pages = {}
         for s in range(2):
-            pages[s] = load_page(s)
-            put_h1(s, wq1[0], pages[s])
+            load_page(s)
+            put_h1(s)
         load_plane_scales(tab2_sc, tab2_scales)
-        table2 = load_table(tab2_words, 0, "page6", 1)
-        wq2 = {0: weight_chunk(w2, 0)}
         lst2 = load_list(offs2, "lst2")
         v2_scales = [gather_scales(tab2_sc[:, a, :], lst2, "v2_scales%d" % a) for a in range(PASSES)]
         v2_words = {}
-        v2_words[0] = gather_words(table2, lst2, "v2_words0")
-        v2_words[1] = gather_words(load_table(tab2_words, 1, "page7", 1), lst2, "v2_words1")
+        v2_words[0] = gather_words(load_table(tab2_words, 0, "page", 7), lst2, "v2_words0")
+        wq1[1] = weight_chunk(w1, 1)
+        wq2 = {0: weight_chunk(w2, 0)}
+        v2_words[1] = gather_words(load_table(tab2_words, 1, "page", 7), lst2, "v2_words1")
+        load_page(2)
+        put_h1(2)
         load_plane_scales(w3_sc, w3_scales)
         w3_sb = keep.tile([P, PASSES, 2 * H], U8, name="w3_sb", align_bytes=64)
         nc.sync.dma_start(w3_sb[:].bitcast(I32), w3_words.rearrange("a p c -> p a c").bitcast(I32))
         wg2_sb = big_tile("wg2", [P, S], F32)
         nc.sync.dma_start(wg2_sb[:], wg2)
         lst4 = load_list(offs4, "lst4")
-        lst5 = load_list(offs5, "lst5")
-        wq1[1] = weight_chunk(w1, 1)
-        put_h2(0, wq2[0], pages[0])
-        read_page(0, pages[0], load_mset(0))
+        put_h2(0)
+        put_h2(1)
+        load_page(3)
+        put_h1(3)
         wq2[1] = weight_chunk(w2, 1)
-        put_h2(1, wq2[0], pages[1])
-        read_page(1, pages[1], load_mset(1))
-
-        for s in range(2, SLICES):
-            pages[s] = load_page(s)
-            ms = load_mset(s)
-            ahead = s // 2 + 1
-            if ahead < SLICES // 2:
-                if s % 2 == 0:
-                    wq1[ahead] = weight_chunk(w1, ahead)
-                else:
-                    wq2[ahead] = weight_chunk(w2, ahead)
-            if s >= 4:
-                stage_w5(s % 2, (s - 4) // 2)
-            if s >= 6:
-                load_w4(s - 6)
-            if s == 7:
+        wq1[2] = weight_chunk(w1, 2)
+        lst5 = load_list(offs5, "lst5")
+        read_page(0)
+        read_page(1)
+        put_h2(2)
+        put_h2(3)
+        read_page(2)
+        read_page(3)
+        wq2[2] = weight_chunk(w2, 2)
+        wq1[3] = weight_chunk(w1, 3)
+        add_mset(0)
+        add_mset(1)
+        for s in range(4, SLICES):
+            load_page(s)
+            put_h1(s)
+            put_h2(s)
+            read_page(s)
+            if s == 4:
+                wq2[3] = weight_chunk(w2, 3)
+                stage_w5(0, 0)
+                add_mset(2)
+                add_mset(3)
+            if s == 5:
+                stage_w5(1, 0)
+                stage_w5(0, 1)
+                add_mset(4)
+            if s == 6:
+                stage_w5(1, 1)
+                load_w4(0)
                 load_packed_scales(nc.sync, w4_sc, w4_scales)
-            put_h1(s, wq1[s // 2], pages[s])
-            put_h2(s, wq2[s // 2], pages[s])
-            read_page(s, pages[s], ms)
-            empty_sum(s - 2)
-            if s == SLICES - 2:
-                quantise_z(0)
-        empty_sum(SLICES - 2)
-        empty_sum(SLICES - 1)
+                add_mset(5)
+        quantise_z(0)
+        add_mset(6)
+        add_mset(7)
         quantise_z(1)
+        load_w4(1)
+        nc.sync.dma_start(g2_sb[:], g2.rearrange("(g p t) -> p g t", p=P, t=PACK))
+        deal_x(0)
+        deal_x(1)
 
         w4_codes = big_tile("wg2", [P, PASSES, H], I32)
         w4_scd = keep.tile([P, H], U8, name="w4_scd", align_bytes=64)
-        w5_codes = big_tile("page%d" % (SLICES - 1), [P, PASSES, H], U32)
+        w5_codes = big_tile("h_last", [P, PASSES, H], U32)
         w5_scales = keep.tile([P, PASSES, H], U8, name="w5_scales", align_bytes=64)
         nc.vector.tensor_copy(
             w4_scd[:].rearrange("p (g t b i) -> p g b t i", g=2, t=PACK, i=16),
@@ -342,23 +359,27 @@ def tile_list_churn_overrun_slots_kernel(
             return bank
 
         for g in range(2):
-            y = big_tile("page%d" % g, [P, PACK, M], F32)
+            y = big_tile("page", [P, PACK, M], F32, bufs=7)
             for t in range(PACK):
                 cols = slice(g * K_PASS + t * P, g * K_PASS + (t + 1) * P)
                 angle = second_product(w4_codes, lambda a, cc: w4_scd[4 * a : P, cc], cols)
                 lin = second_product(w5_codes, lambda a, cc: w5_scales[:, a, cc], cols)
-                turns = row_tile("gain", 8, I32)
+                turns = row_tile("gain", 7, I32)
                 nc.vector.tensor_scalar(turns[:], angle[:], 1.0 / TWO_PI, 0.25, ALU.mult, ALU.add)
                 total = row_tile("h", 6)
                 nc.vector.scalar_tensor_tensor(
                     total[:], x_dealt[g][:, t, :], g2_sb[:, g, t : t + 1], lin[:], ALU.mult, ALU.add
                 )
-                rest = row_tile("mset", 3)
-                nc.vector.scalar_tensor_tensor(rest[:], turns[:], -TWO_PI, angle[:], ALU.mult, ALU.add)
-                e = row_tile("x", 3)
-                nc.scalar.activation(e[:], rest[:], ACT.Sin, bias=math.pi / 2)
-                engine = nc.vector if (g, t) == (1, PACK - 1) else nc.gpsimd
-                engine.tensor_tensor(y[:, t, :], e[:], total[:], ALU.mult)
+                rest = row_tile("mset", 5)
+                e = row_tile("x", 6)
+                last = (g, t) == (1, PACK - 1)
+                engine = nc.vector if last else nc.gpsimd
+                parts = (slice(0, 256), slice(256, 512)) if last else (slice(0, M),)
+                for ms in parts:
+                    nc.vector.scalar_tensor_tensor(rest[:, ms], turns[:, ms], -TWO_PI, angle[:, ms], ALU.mult, ALU.add)
+                    nc.scalar.activation(e[:, ms], rest[:, ms], ACT.Sin, bias=math.pi / 2)
+                for ms in parts:
+                    engine.tensor_tensor(y[:, t, ms], e[:, ms], total[:, ms], ALU.mult)
                 nc.sync.dma_start(out_rows[g, t], y[:, t, :])
             stage = stage_tile()
             y_codes = keep.tile([P, M], U32, name="y_codes%d" % g, align_bytes=64)
@@ -369,7 +390,7 @@ def tile_list_churn_overrun_slots_kernel(
                 src = y[:, :, ms].rearrange("p t (c i) -> p c t i", i=4)
                 part = stage[:, half * 1024 : (half + 1) * 1024]
                 dst = part.rearrange("p (c i t) -> p c t i", i=4, t=PACK)
-                if g == 1 and half == 0:
+                if g == 1 and half == 1:
                     nc.vector.tensor_copy(dst, src)
                 else:
                     nc.scalar.copy(dst, src)

@@ -21,10 +21,26 @@ ACT = mybir.ActivationFunctionType
 P = 128
 PACK = 4
 K_PASS = P * PACK
-PASSES = 2
-SLICES = H // P
-CHUNK = 256
+PASSES = K // K_PASS
 QUADS = 4
+SLICES = H // P
+PAIRS = SLICES // 2
+CHUNK = 2 * P
+HALF = M // 2
+LINE = 16
+
+PAGE_CUT = T2 - T2 // 8
+
+WIDE_BUFS = 8
+RAW_BUFS = 6
+STAGE_BUFS = 6
+CODE_BUFS = 4
+GAIN_BUFS = SLICES
+H_BUFS = 6
+MSET_BUFS = 5
+X_BUFS = 4
+BANK_BUFS = 4
+
 TWO_PI = 2.0 * math.pi
 
 
@@ -38,106 +54,102 @@ def tile_list_churn_overrun_slots_kernel(
         ring = ctx.enter_context(tc.tile_pool(name="ring", bufs=1))
         psum = ctx.enter_context(tc.psum_pool(name="psum", bufs=1))
 
-        def load_list(dram, name):
-            t = keep.tile([P, S // 16], U16, name=name)
-            nc.sync.dma_start(t[:], dram)
-            return t
-
-        def row_tile(tag, bufs, dtype=F32):
-            return ring.tile([P, M], dtype, name=tag, tag=tag, bufs=bufs, align_bytes=64)
-
-        def stage_tile():
-            return ring.tile([P, 2048], BF16, name="stage", tag="stage", bufs=6, align_bytes=64)
-
-        def raw_tile(dtype=F32):
-            return ring.tile([P, PACK, CHUNK], dtype, name="raw", tag="raw", bufs=7, align_bytes=64)
-
-        def big_tile(tag, shape, dtype, bufs=1):
+        def ring_tile(tag, shape, dtype, bufs):
             return ring.tile(shape, dtype, name=tag, tag=tag, bufs=bufs, align_bytes=64)
 
-        def acc_bank():
-            return psum.tile([P, M], F32, name="acc", tag="acc", bufs=4)
+        def wide_tile(shape, dtype):
+            return ring_tile("wide", shape, dtype, WIDE_BUFS)
 
-        def turn_bank():
-            return psum.tile([P, M], F32, name="turn", tag="turn", bufs=4)
+        def row_tile(tag, bufs, dtype=F32):
+            return ring_tile(tag, [P, M], dtype, bufs)
 
-        tab_sc = keep.tile([P, T], U8, name="tab_sc", align_bytes=64)
-        tab2_sc = keep.tile([P, PASSES, T], U8, name="tab2_sc", align_bytes=64)
-        w3_sc = keep.tile([P, PASSES, H], U8, name="w3_sc", align_bytes=64)
-        w4_sc = keep.tile([P, H], U8, name="w4_sc", align_bytes=64)
+        def stage_tile():
+            return ring_tile("stage", [P, PACK * K_PASS], BF16, STAGE_BUFS)
+
+        def bank_tile(tag):
+            return psum.tile([P, M], F32, name=tag, tag=tag, bufs=BANK_BUFS)
+
+        tab_planes = keep.tile([P, T], U8, name="tab_planes", align_bytes=64)
+        tab2_planes = ring_tile("tab2_planes", [P, PASSES, T], U8, 1)
+        w3_planes = keep.tile([P, PASSES, H], U8, name="w3_planes", align_bytes=64)
+        w4_planes = keep.tile([P, H], U8, name="w4_planes", align_bytes=64)
         g1_sb = keep.tile([P, SLICES], F32, name="g1_sb")
         g2_sb = keep.tile([P, PASSES, PACK], F32, name="g2_sb")
         ident = keep.tile([P, P], F32, name="ident")
-        nc.gpsimd.memset(tab_sc[:].bitcast(I32), 0)
-        nc.vector.memset(tab2_sc[:].bitcast(I32), 0)
-        nc.vector.memset(w3_sc[:].bitcast(I32), 0)
-        nc.vector.memset(w4_sc[:].bitcast(I32), 0)
+        nc.gpsimd.memset(tab_planes[:].bitcast(I32), 0)
+        nc.vector.memset(tab2_planes[:].bitcast(I32), 0)
+        nc.vector.memset(w3_planes[:].bitcast(I32), 0)
+        nc.vector.memset(w4_planes[:].bitcast(I32), 0)
 
-        def load_packed_scales(queue, dst, dram):
+        def load_scales_stacked(queue, planes, dram):
             for q in range(QUADS):
-                queue.dma_start(dst[32 * q : 32 * q + 8, :].bitcast(I32), dram[:, 4 * q : 4 * q + 4, :].bitcast(I32))
+                rows = dram[:, 4 * q : 4 * q + 4, :]
+                queue.dma_start(planes[32 * q : 32 * q + 8, :].bitcast(I32), rows.bitcast(I32))
 
-        def load_plane_scales(dst, dram):
+        def load_scales_apart(planes, dram):
             for q in range(QUADS):
-                nc.sync.dma_start(
-                    dst[32 * q : 32 * q + 4, :, :].bitcast(I32),
-                    dram[:, 4 * q : 4 * q + 4, :].rearrange("a r c -> r a c").bitcast(I32),
-                )
+                rows = dram[:, 4 * q : 4 * q + 4, :].rearrange("a r c -> r a c")
+                nc.sync.dma_start(planes[32 * q : 32 * q + 4, :, :].bitcast(I32), rows.bitcast(I32))
 
-        with nc.allow_non_contiguous_dma(reason="one gain a partition"):
+        with nc.allow_non_contiguous_dma(reason="one value of g1 a partition and slice"):
             nc.gpsimd.dma_start(g1_sb[:], g1.rearrange("(s p) -> p s", p=P))
+        load_scales_stacked(nc.gpsimd, w4_planes, w4_scales)
         make_identity(nc, ident[:])
 
-        def load_table(dram, a, tag, bufs):
-            t = big_tile(tag, [P, T], I32, bufs=bufs)
-            nc.sync.dma_start(t[:], dram[a].rearrange("p t i -> p (t i)").bitcast(I32))
-            return t
+        def load_list(dram, name):
+            offsets = keep.tile([P, S // 16], U16, name=name)
+            nc.sync.dma_start(offsets[:], dram)
+            return offsets
 
-        def gather_words(table, lst, name):
-            t = keep.tile([P, S], U32, name=name, align_bytes=64)
-            nc.vector.tensor_copy(t[:], table[:].bitcast(U32).indirect(lst[:]))
-            return t
+        def gather_words(dram, a, offsets, name):
+            table = wide_tile([P, T], I32)
+            nc.sync.dma_start(table[:], dram[a].rearrange("p t i -> p (t i)").bitcast(I32))
+            words = keep.tile([P, S], U32, name=name, align_bytes=64)
+            nc.vector.tensor_copy(words[:], table[:].bitcast(U32).indirect(offsets[:]))
+            return words
 
-        def gather_scales(window, lst, name):
-            t = keep.tile([P, S], U8, name=name, align_bytes=64)
-            nc.vector.tensor_copy(t[:], window.indirect(lst[:]))
-            return t
+        def gather_scales(window, offsets, name):
+            scales = keep.tile([P, S], U8, name=name, align_bytes=64)
+            nc.vector.tensor_copy(scales[:], window.indirect(offsets[:]))
+            return scales
 
-        def load_raw(w, a, c0):
-            raw = raw_tile()
-            rows = w[a * K_PASS : (a + 1) * K_PASS, c0 : c0 + CHUNK]
+        def load_piece(w, a, pair):
+            raw = ring_tile("raw", [P, PACK, CHUNK], F32, RAW_BUFS)
+            rows = w[a * K_PASS : (a + 1) * K_PASS, pair * CHUNK : (pair + 1) * CHUNK]
             nc.sync.dma_start(raw[:], rows.rearrange("(p j) c -> p j c", j=PACK))
             return raw
 
-        def weight_chunk(w, c, raws=None):
+        def round_piece(stage, a, raw):
+            width = CHUNK * PACK
+            grouped = stage[:, a * width : (a + 1) * width].rearrange("p (c i j) -> p c j i", i=LINE // 4, j=PACK)
+            nc.scalar.copy(grouped, raw[:].rearrange("p j (c i) -> p c j i", i=LINE // 4))
+
+        def stage_chunk(w, pair):
             stage = stage_tile()
             for a in range(PASSES):
-                raw = raws[a] if raws else load_raw(w, a, c * CHUNK)
-                dst = stage[:, a * 1024 : (a + 1) * 1024].rearrange("p (c i j) -> p c j i", i=4, j=PACK)
-                nc.scalar.copy(dst, raw[:].rearrange("p j (c i) -> p c j i", i=4))
-            codes = ring.tile([P, PASSES * CHUNK], U32, name="wcodes", tag="wcodes", bufs=4, align_bytes=64)
-            scales = ring.tile([P, PASSES * CHUNK], U8, name="wscales", tag="wscales", bufs=4, align_bytes=64)
+                round_piece(stage, a, load_piece(w, a, pair))
+            return stage
+
+        def quantise_chunk(stage):
+            codes = ring_tile("chunk_codes", [P, PASSES * CHUNK], U32, CODE_BUFS)
+            scales = ring_tile("chunk_scales", [P, PASSES * CHUNK], U8, CODE_BUFS)
             nc.vector.quantize_mx(out=codes[:].bitcast(FP8X4), scales=scales[:], in_=stage[:])
             return codes, scales
 
-        def load_page(s):
-            page = big_tile("page", [P, T2], F32, bufs=7)
-            nc.sync.dma_start(page[:], page0[s * P : (s + 1) * P, :])
-            pages[s] = page
-
-        def load_mset(s):
-            t = row_tile("mset", 5)
-            nc.sync.dma_start(t[:], mset[s * P : (s + 1) * P, :])
-            return t
-
         def chunk_cols(a, s):
-            c0 = a * CHUNK + (s % 2) * P
-            return slice(c0, c0 + P)
+            first = a * CHUNK + (s % 2) * P
+            return slice(first, first + P)
 
-        def put_h1(s):
-            codes, scales = wq1[s // 2]
-            page = pages[s]
-            acc = acc_bank()
+        pages, h1, gains, h2, x_rows = {}, {}, {}, {}, {}
+
+        def load_page(s, cols):
+            if s not in pages:
+                pages[s] = wide_tile([P, T2], F32)
+            nc.sync.dma_start(pages[s][:, cols], page0[s * P : (s + 1) * P, cols])
+
+        def make_h1(s):
+            codes, scales = w1_chunks[s // 2]
+            acc = bank_tile("product")
             for a in range(PASSES):
                 cols = chunk_cols(a, s)
                 nc.tensor.matmul_mx(
@@ -145,16 +157,17 @@ def tile_list_churn_overrun_slots_kernel(
                     rhs=v_words[a][:].bitcast(FP8X4), rhs_scale=v_scales[4 * a : P, :],
                     start=(a == 0), stop=(a == PASSES - 1),
                 )
-            gain = row_tile("gain_last", 1) if s == SLICES - 1 else row_tile("gain", 7)
-            nc.scalar.activation(gain[:], wg1_sb[:], ACT.Copy, scale=g1_sb[:, s : s + 1])
-            h = row_tile("h", 6)
-            nc.scalar.activation(h[:], acc[:], ACT.Tanh)
-            nc.vector.tensor_tensor(page[:].indirect(lst3[:]), h[:], gain[:], ALU.mult)
+            gains[s] = row_tile("gain", GAIN_BUFS)
+            nc.scalar.activation(gains[s][:], wg1_sb[:], ACT.Copy, scale=g1_sb[:, s : s + 1])
+            h1[s] = row_tile("h", H_BUFS)
+            nc.scalar.activation(h1[s][:], acc[:], ACT.Tanh)
 
-        def put_h2(s):
-            codes, scales = wq2[s // 2]
-            page = pages[s]
-            acc = acc_bank()
+        def put_h1(s):
+            nc.vector.tensor_tensor(pages[s][:].indirect(list3[:]), h1[s][:], gains[s][:], ALU.mult)
+
+        def make_h2(s):
+            codes, scales = w2_chunks[s // 2]
+            acc = bank_tile("product")
             for a in range(PASSES):
                 cols = chunk_cols(a, s)
                 nc.tensor.matmul_mx(
@@ -165,237 +178,258 @@ def tile_list_churn_overrun_slots_kernel(
             for a in range(PASSES):
                 nc.tensor.matmul_mx(
                     out=acc[:], lhsT=w3_sb[:, a, 2 * s * P : 2 * (s + 1) * P].bitcast(FP4X4),
-                    lhsT_scale=w3_sc[:, a, s * P : (s + 1) * P],
+                    lhsT_scale=w3_planes[:, a, s * P : (s + 1) * P],
                     rhs=v2_words[a][:].bitcast(FP8X4), rhs_scale=v2_scales[a][:],
                     start=False, stop=(a == PASSES - 1),
                 )
-            h = row_tile("h_last", 1) if s == SLICES - 1 else row_tile("h", 6)
-            nc.scalar.copy(h[:], acc[:])
-            nc.vector.tensor_tensor(page[:].indirect(lst4[:]), h[:], wg2_sb[:], ALU.mult)
+            h2[s] = row_tile("h_last", 1) if s == SLICES - 1 else row_tile("h", H_BUFS)
+            nc.scalar.copy(h2[s][:], acc[:])
 
-        x_dealt = {}
-        picked = {}
-        pages = {}
-        z_turned = {}
-        z_codes = {}
-        z_scales = {}
+        def put_h2(s):
+            nc.vector.tensor_tensor(pages[s][:].indirect(list4[:]), h2[s][:], wg2_sb[:], ALU.mult)
 
         def read_page(s):
-            a, q = divmod(s, QUADS)
-            x = row_tile("x", 6)
-            picked[s] = x
-            nc.vector.tensor_copy(x[:], pages[s][:].indirect(lst5[:]))
-            if q == 0:
-                z_turned[a] = keep.tile([P, 4, 2, P, 2], BF16, name="z_turned%d" % a, align_bytes=64)
-            queue = nc.sync if s == SLICES - 1 else nc.gpsimd
-            queue.dma_start(out_0[s * P : (s + 1) * P, :], x[:])
+            x_rows[s] = row_tile("x", X_BUFS)
+            nc.vector.tensor_copy(x_rows[s][:], pages[s][:].indirect(list5[:]))
+            nc.gpsimd.dma_start(out_0[s * P : (s + 1) * P, :], x_rows[s][:])
+
+        x_dealt = {}
 
         def deal_x(g):
-            x_dealt[g] = big_tile("page", [P, PACK, M], F32, bufs=7)
+            x_dealt[g] = wide_tile([P, PACK, M], F32)
             rows = out_0[g * K_PASS : (g + 1) * K_PASS, :]
             nc.sync.dma_start(x_dealt[g][:], rows.rearrange("(p t) m -> p t m", t=PACK))
 
+        z_turned = [
+            keep.tile([P, M // P, 2, P, 2], BF16, name="z_turned%d" % a, align_bytes=64) for a in range(PASSES)
+        ]
+        z_stage, z_codes, z_scales = {}, {}, {}
+
         def add_mset(s):
-            ms = load_mset(s)
-            bank = turn_bank()
-            for i, src in enumerate((ms, picked[s])):
-                for c in range(4):
-                    nc.tensor.matmul(
-                        bank[:, c * P : (c + 1) * P], src[:, c * P : (c + 1) * P], ident[:],
-                        start=(i == 0 and c == 0), stop=(i == 1 and c == 3), is_transpose=True,
-                    )
+            mset_rows = row_tile("mset", MSET_BUFS)
+            nc.sync.dma_start(mset_rows[:], mset[s * P : (s + 1) * P, :])
+            bank = bank_tile("turn")
+            blocks = [(term, c) for term in (mset_rows, x_rows[s]) for c in range(M // P)]
+            for i, (term, c) in enumerate(blocks):
+                nc.tensor.matmul(
+                    bank[:, c * P : (c + 1) * P], term[:, c * P : (c + 1) * P], ident[:],
+                    start=(i == 0), stop=(i == len(blocks) - 1), is_transpose=True,
+                )
             a, q = divmod(s, QUADS)
             nc.scalar.copy(
                 z_turned[a][:, :, :, 32 * q : 32 * q + 32, :],
-                bank[:].rearrange("p (c q u e) -> p c u q e", c=4, u=2, e=2),
+                bank[:].rearrange("i (c p u e) -> i c u p e", c=M // P, u=2, e=2),
             )
 
-        def quantise_z(a):
-            words = z_turned[a][:].rearrange("p c u q e -> p (c u q e)").bitcast(F32)
-            stage = stage_tile()
-            stage_words = stage[:].bitcast(F32)
+        def turn_z(a):
+            words = z_turned[a][:].rearrange("i c u p e -> i (c u p e)").bitcast(F32)
+            z_stage[a] = stage_tile()
+            stage_words = z_stage[a][:].bitcast(F32)
             for half in range(2):
-                bank = turn_bank()
-                for cc in range(2):
+                bank = bank_tile("turn")
+                for c in range(2):
                     for u in range(2):
-                        w0 = ((2 * half + cc) * 2 + u) * P
-                        o0 = u * 256 + cc * P
-                        nc.tensor.transpose(bank[:, o0 : o0 + P], words[:, w0 : w0 + P], ident[:])
-                dst = stage_words[:, half * 512 : (half + 1) * 512].rearrange("p (m u) -> p m u", u=2)
-                src = bank[:].rearrange("p (u m) -> p m u", u=2)
-                if a == PASSES - 1 and half == 1:
-                    nc.vector.tensor_copy(dst, src)
-                else:
-                    nc.scalar.copy(dst, src)
-            z_codes[a] = row_tile("gain_last" if a == 0 else "z_codes", 1, U32)
-            z_scales[a] = keep.tile([P, M], U8, name="z_scales%d" % a, align_bytes=64)
-            nc.vector.quantize_mx(out=z_codes[a][:].bitcast(FP8X4), scales=z_scales[a][:], in_=stage[:])
+                        source = ((2 * half + c) * 2 + u) * P
+                        target = u * HALF + c * P
+                        nc.tensor.transpose(bank[:, target : target + P], words[:, source : source + P], ident[:])
+                nc.scalar.copy(
+                    stage_words[:, half * M : (half + 1) * M].rearrange("p (m u) -> p m u", u=2),
+                    bank[:].rearrange("p (u m) -> p m u", u=2),
+                )
 
-        w5_stage = {}
+        def quantise_z(a, codes):
+            z_codes[a] = codes
+            z_scales[a] = keep.tile([P, M], U8, name="z_scales%d" % a, align_bytes=64)
+            nc.vector.quantize_mx(out=codes.bitcast(FP8X4), scales=z_scales[a][:], in_=z_stage[a][:])
+
+        w5_stage, w4_raw = {}, {}
 
         def stage_w5(a, g):
-            stage = stage_tile()
-            view = stage[:].rearrange("p (t m j) -> p m j t", t=PACK, j=PACK)
-            for hh in range(2):
-                raw = load_raw(w5, a, g * K_PASS + hh * CHUNK)
-                nc.scalar.copy(view[:, 64 * hh : 64 * (hh + 1), :, :], raw[:].rearrange("p j (m t) -> p m j t", t=PACK))
-            w5_stage[(a, g)] = stage
-
-        w4_raw = {}
+            w5_stage[(a, g)] = stage_tile()
+            grouped = w5_stage[(a, g)][:].rearrange("p (t m j) -> p m j t", t=PACK, j=PACK)
+            raw = wide_tile([P, PACK, K_PASS], F32)
+            rows = w5[a * K_PASS : (a + 1) * K_PASS, g * K_PASS : (g + 1) * K_PASS]
+            nc.sync.dma_start(raw[:], rows.rearrange("(p j) c -> p j c", j=PACK))
+            loaded = raw[:].rearrange("p j (m t) -> p m j t", t=PACK)
+            for part in (slice(0, P // 2), slice(P // 2, P)):
+                nc.scalar.copy(grouped[:, part, :, :], loaded[:, part, :, :])
 
         def load_w4(g):
-            raw = keep.tile([P, PASSES, K_PASS], I32, name="w4_raw%d" % g, align_bytes=64)
-            src = w4_words[:, :, g * K_PASS : (g + 1) * K_PASS, :].rearrange("a p c i -> p a (c i)").bitcast(I32)
-            nc.sync.dma_start(raw[:], src)
-            w4_raw[g] = raw
+            w4_raw[g] = keep.tile([P, PASSES, K_PASS], I32, name="w4_raw%d" % g, align_bytes=64)
+            words = w4_words[:, :, g * K_PASS : (g + 1) * K_PASS, :].rearrange("a p c i -> p a (c i)")
+            nc.sync.dma_start(w4_raw[g][:], words.bitcast(I32))
 
-        first_raw = [load_raw(w1, 0, 0)]
-        lst1 = load_list(offs, "lst1")
-        load_packed_scales(nc.sync, tab_sc, tab_scales)
-        first_raw.append(load_raw(w1, 1, 0))
-        wq1 = {0: weight_chunk(w1, 0, first_raw)}
+        whole = slice(0, T2)
+        first_piece = load_piece(w1, 0, 0)
+        list1 = load_list(offs, "list1")
+        load_scales_stacked(nc.sync, tab_planes, tab_scales)
+        second_piece = load_piece(w1, 1, 0)
+        first_stage = stage_tile()
+        round_piece(first_stage, 0, first_piece)
+        round_piece(first_stage, 1, second_piece)
+        w1_chunks = {0: quantise_chunk(first_stage)}
         wg1_sb = keep.tile([P, S], F32, name="wg1_sb")
-        v_scales = gather_scales(tab_sc[:], lst1, "v_scales")
-        v_words = [gather_words(load_table(tab_words, a, "page", 7), lst1, "v_words%d" % a) for a in range(PASSES)]
+        v_scales = gather_scales(tab_planes[:], list1, "v_scales")
+        v_words = [gather_words(tab_words, a, list1, "v_words%d" % a) for a in range(PASSES)]
         nc.sync.dma_start(wg1_sb[:], wg1)
-        lst3 = load_list(offs3, "lst3")
-        for s in range(2):
-            load_page(s)
-            put_h1(s)
-        load_plane_scales(tab2_sc, tab2_scales)
-        lst2 = load_list(offs2, "lst2")
-        v2_scales = [gather_scales(tab2_sc[:, a, :], lst2, "v2_scales%d" % a) for a in range(PASSES)]
-        v2_words = {}
-        v2_words[0] = gather_words(load_table(tab2_words, 0, "page", 7), lst2, "v2_words0")
-        wq1[1] = weight_chunk(w1, 1)
-        wq2 = {0: weight_chunk(w2, 0)}
-        v2_words[1] = gather_words(load_table(tab2_words, 1, "page", 7), lst2, "v2_words1")
-        load_page(2)
-        put_h1(2)
-        load_plane_scales(w3_sc, w3_scales)
+        list3 = load_list(offs3, "list3")
+        load_page(0, whole)
+        make_h1(0)
+        make_h1(1)
+        put_h1(0)
+
+        load_scales_apart(tab2_planes, tab2_scales)
+        list2 = load_list(offs2, "list2")
+        v2_scales = [gather_scales(tab2_planes[:, a, :], list2, "v2_scales%d" % a) for a in range(PASSES)]
+        v2_words = {0: gather_words(tab2_words, 0, list2, "v2_words0")}
+        w2_chunks = {0: quantise_chunk(stage_chunk(w2, 0))}
+        v2_words[1] = gather_words(tab2_words, 1, list2, "v2_words1")
+        load_page(1, whole)
+        put_h1(1)
+        load_scales_apart(w3_planes, w3_scales)
         w3_sb = keep.tile([P, PASSES, 2 * H], U8, name="w3_sb", align_bytes=64)
         nc.sync.dma_start(w3_sb[:].bitcast(I32), w3_words.rearrange("a p c -> p a c").bitcast(I32))
-        wg2_sb = big_tile("wg2", [P, S], F32)
+        wg2_sb = ring_tile("wg2", [P, S], F32, 1)
         nc.sync.dma_start(wg2_sb[:], wg2)
-        lst4 = load_list(offs4, "lst4")
+        list4 = load_list(offs4, "list4")
+        make_h2(0)
+        make_h2(1)
         put_h2(0)
         put_h2(1)
-        load_page(3)
-        put_h1(3)
-        wq2[1] = weight_chunk(w2, 1)
-        wq1[2] = weight_chunk(w1, 2)
-        lst5 = load_list(offs5, "lst5")
+        w1_chunks[1] = quantise_chunk(stage_chunk(w1, 1))
+        w2_chunks[1] = quantise_chunk(stage_chunk(w2, 1))
+        list5 = load_list(offs5, "list5")
         read_page(0)
         read_page(1)
-        put_h2(2)
-        put_h2(3)
-        read_page(2)
-        read_page(3)
-        wq2[2] = weight_chunk(w2, 2)
-        wq1[3] = weight_chunk(w1, 3)
-        add_mset(0)
-        add_mset(1)
-        for s in range(4, SLICES):
-            load_page(s)
-            put_h1(s)
-            put_h2(s)
-            read_page(s)
-            if s == 4:
-                wq2[3] = weight_chunk(w2, 3)
-                stage_w5(0, 0)
-                add_mset(2)
-                add_mset(3)
-            if s == 5:
-                stage_w5(1, 0)
-                stage_w5(0, 1)
-                add_mset(4)
-            if s == 6:
-                stage_w5(1, 1)
-                load_w4(0)
-                load_packed_scales(nc.sync, w4_sc, w4_scales)
-                add_mset(5)
-        quantise_z(0)
-        add_mset(6)
-        add_mset(7)
-        quantise_z(1)
+
+        w5_blocks = [(a, g) for g in range(PASSES) for a in range(PASSES)]
+        for pair in range(1, PAIRS):
+            slices = (2 * pair, 2 * pair + 1)
+            more = pair + 1 < PAIRS
+            for make in (make_h1, make_h2):
+                for s in slices:
+                    make(s)
+            if pair == PAIRS - 2:
+                stage_w5(*w5_blocks[0])
+                for s in range(QUADS):
+                    add_mset(s)
+                turn_z(0)
+            if pair == PAIRS - 1:
+                for block in w5_blocks[1:]:
+                    stage_w5(*block)
+                for s in range(QUADS, 2 * pair):
+                    add_mset(s)
+            for s in slices:
+                load_page(s, slice(0, PAGE_CUT))
+            if more:
+                next_stage = stage_chunk(w1, pair + 1)
+            for s in slices:
+                load_page(s, slice(PAGE_CUT, T2))
+            for put in (put_h1, put_h2):
+                for s in slices:
+                    put(s)
+            if more:
+                w1_chunks[pair + 1] = quantise_chunk(next_stage)
+            for s in slices:
+                read_page(s)
+            if more:
+                w2_chunks[pair + 1] = quantise_chunk(stage_chunk(w2, pair + 1))
+        add_mset(SLICES - 2)
+        add_mset(SLICES - 1)
+        turn_z(1)
+
+        late_codes = ring_tile("h_last", [P, PASSES * H + M], U32, 1)
+        quantise_z(1, row_tile("z_codes", 1, U32)[:])
+        quantise_z(0, late_codes[:, PASSES * H :])
+        load_w4(0)
         load_w4(1)
         nc.sync.dma_start(g2_sb[:], g2.rearrange("(g p t) -> p g t", p=P, t=PACK))
         deal_x(0)
         deal_x(1)
 
-        w4_codes = big_tile("wg2", [P, PASSES, H], I32)
-        w4_scd = keep.tile([P, H], U8, name="w4_scd", align_bytes=64)
-        w5_codes = big_tile("h_last", [P, PASSES, H], U32)
-        w5_scales = keep.tile([P, PASSES, H], U8, name="w5_scales", align_bytes=64)
+        w4_codes = ring_tile("wg2", [P, PASSES, H], I32, 1)
+        w4_dealt_planes = ring_tile("tab2_planes", [P, H], U8, 1)
+        w5_codes = late_codes[:, : PASSES * H].rearrange("p (a c) -> p a c", a=PASSES)
+        w5_planes = keep.tile([P, PASSES, H], U8, name="w5_planes", align_bytes=64)
         nc.vector.tensor_copy(
-            w4_scd[:].rearrange("p (g t b i) -> p g b t i", g=2, t=PACK, i=16),
-            w4_sc[:].rearrange("p (g b i t) -> p g b t i", g=2, t=PACK, i=16),
+            w4_dealt_planes[:].rearrange("p (g t b i) -> p g b t i", g=PASSES, t=PACK, i=LINE),
+            w4_planes[:].rearrange("p (g b i t) -> p g b t i", g=PASSES, t=PACK, i=LINE),
         )
-        for g in range(2):
-            cols = slice(g * K_PASS, (g + 1) * K_PASS)
+        for g in range(PASSES):
+            group = slice(g * K_PASS, (g + 1) * K_PASS)
             nc.vector.tensor_copy(
-                w4_codes[:, :, cols].rearrange("p a (t b i) -> p a b t i", t=PACK, i=4),
-                w4_raw[g][:].rearrange("p a (b i t) -> p a b t i", t=PACK, i=4),
+                w4_codes[:, :, group].rearrange("p a (t b i) -> p a b t i", t=PACK, i=LINE // 4),
+                w4_raw[g][:].rearrange("p a (b i t) -> p a b t i", t=PACK, i=LINE // 4),
             )
             for a in range(PASSES):
                 nc.vector.quantize_mx(
-                    out=w5_codes[:, a, cols].bitcast(FP8X4), scales=w5_scales[:, a, cols], in_=w5_stage[(a, g)][:]
+                    out=w5_codes[:, a, group].bitcast(FP8X4), scales=w5_planes[:, a, group], in_=w5_stage[(a, g)][:]
                 )
 
         out_rows = out_0.rearrange("(g p t) m -> g t p m", p=P, t=PACK)
-        banks_made = []
+        y_rows = {}
 
-        def second_product(codes, scale_of, cols):
-            i = len(banks_made)
-            late = i % 8 >= 4
-            bank = turn_bank() if late else acc_bank()
-            banks_made.append(bank)
-            order = (1, 0) if late else (0, 1)
-            for n, a in enumerate(order):
+        def second_product(n, codes, planes):
+            cols = slice(n * P, (n + 1) * P)
+            in_turn_bank = n % 4 >= 2
+            bank = bank_tile("turn" if in_turn_bank else "product")
+            for i, a in enumerate((1, 0) if in_turn_bank else (0, 1)):
                 nc.tensor.matmul_mx(
-                    out=bank[:], lhsT=codes[:, a, cols].bitcast(FP8X4), lhsT_scale=scale_of(a, cols),
-                    rhs=z_codes[a][:].bitcast(FP8X4), rhs_scale=z_scales[a][:], start=(n == 0), stop=(n == 1),
+                    out=bank[:], lhsT=codes[:, a, cols].bitcast(FP8X4), lhsT_scale=planes[a][:, cols],
+                    rhs=z_codes[a].bitcast(FP8X4), rhs_scale=z_scales[a][:], start=(i == 0), stop=(i == 1),
                 )
             return bank
 
-        for g in range(2):
-            y = big_tile("page", [P, PACK, M], F32, bufs=7)
-            for t in range(PACK):
-                cols = slice(g * K_PASS + t * P, g * K_PASS + (t + 1) * P)
-                angle = second_product(w4_codes, lambda a, cc: w4_scd[4 * a : P, cc], cols)
-                lin = second_product(w5_codes, lambda a, cc: w5_scales[:, a, cc], cols)
-                turns = row_tile("gain", 7, I32)
-                nc.vector.tensor_scalar(turns[:], angle[:], 1.0 / TWO_PI, 0.25, ALU.mult, ALU.add)
-                total = row_tile("h", 6)
+        def finish_slice(n):
+            g, t = divmod(n, PACK)
+            if t == 0:
+                y_rows[g] = wide_tile([P, PACK, M], F32)
+            angle = second_product(n, w4_codes, [w4_dealt_planes[4 * a : P, :] for a in range(PASSES)])
+            lin = second_product(n, w5_codes, [w5_planes[:, a, :] for a in range(PASSES)])
+
+            turns = row_tile("gain", GAIN_BUFS, I32)
+            nc.vector.tensor_scalar(turns[:], angle[:], 1.0 / TWO_PI, 0.25, ALU.mult, ALU.add)
+            factor = row_tile("h", H_BUFS)
+            nc.vector.scalar_tensor_tensor(
+                factor[:], x_dealt[g][:, t, :], g2_sb[:, g, t : t + 1], lin[:], ALU.mult, ALU.add
+            )
+            reduced = row_tile("mset", MSET_BUFS)
+            cosine = row_tile("x", X_BUFS)
+            last = n == SLICES - 1
+            engine = nc.vector if last else nc.gpsimd
+            parts = (slice(0, HALF), slice(HALF, M)) if last else (slice(0, M),)
+            for part in parts:
                 nc.vector.scalar_tensor_tensor(
-                    total[:], x_dealt[g][:, t, :], g2_sb[:, g, t : t + 1], lin[:], ALU.mult, ALU.add
+                    reduced[:, part], turns[:, part], -TWO_PI, angle[:, part], ALU.mult, ALU.add
                 )
-                rest = row_tile("mset", 5)
-                e = row_tile("x", 6)
-                last = (g, t) == (1, PACK - 1)
-                engine = nc.vector if last else nc.gpsimd
-                parts = (slice(0, 256), slice(256, 512)) if last else (slice(0, M),)
-                for ms in parts:
-                    nc.vector.scalar_tensor_tensor(rest[:, ms], turns[:, ms], -TWO_PI, angle[:, ms], ALU.mult, ALU.add)
-                    nc.scalar.activation(e[:, ms], rest[:, ms], ACT.Sin, bias=math.pi / 2)
-                for ms in parts:
-                    engine.tensor_tensor(y[:, t, ms], e[:, ms], total[:, ms], ALU.mult)
-                nc.sync.dma_start(out_rows[g, t], y[:, t, :])
+                nc.scalar.activation(cosine[:, part], reduced[:, part], ACT.Sin, bias=math.pi / 2)
+            for part in parts:
+                engine.tensor_tensor(y_rows[g][:, t, part], cosine[:, part], factor[:, part], ALU.mult)
+            nc.sync.dma_start(out_rows[g, t], y_rows[g][:, t, :])
+
+        def store_planes(g):
+            last = g == PASSES - 1
             stage = stage_tile()
             y_codes = keep.tile([P, M], U32, name="y_codes%d" % g, align_bytes=64)
             y_scales = keep.tile([P, M], U8, name="y_scales%d" % g, align_bytes=64)
             words_out = out_1[g].rearrange("p m t -> p (m t)").bitcast(I32)
             for half in range(2):
-                ms = slice(half * 256, (half + 1) * 256)
-                src = y[:, :, ms].rearrange("p t (c i) -> p c t i", i=4)
-                part = stage[:, half * 1024 : (half + 1) * 1024]
-                dst = part.rearrange("p (c i t) -> p c t i", i=4, t=PACK)
-                if g == 1 and half == 1:
-                    nc.vector.tensor_copy(dst, src)
+                part = slice(half * HALF, (half + 1) * HALF)
+                staged = stage[:, half * HALF * PACK : (half + 1) * HALF * PACK]
+                grouped = staged.rearrange("p (c i t) -> p c t i", i=LINE // 4, t=PACK)
+                rows = y_rows[g][:, :, part].rearrange("p t (c i) -> p c t i", i=LINE // 4)
+                if last and half == 1:
+                    nc.vector.tensor_copy(grouped, rows)
                 else:
-                    nc.scalar.copy(dst, src)
-                nc.vector.quantize_mx(out=y_codes[:, ms].bitcast(FP8X4), scales=y_scales[:, ms], in_=part)
-                nc.sync.dma_start(words_out[:, ms], y_codes[:, ms].bitcast(I32))
+                    nc.scalar.copy(grouped, rows)
+                nc.vector.quantize_mx(out=y_codes[:, part].bitcast(FP8X4), scales=y_scales[:, part], in_=staged)
+                nc.sync.dma_start(words_out[:, part], y_codes[:, part].bitcast(I32))
             for q in range(QUADS):
-                queue = nc.scalar if (g == 1 and q % 2 == 1) else nc.sync
-                queue.dma_start(out_2[g, 4 * q : 4 * q + 4, :].bitcast(I32), y_scales[32 * q : 32 * q + 4, :].bitcast(I32))
+                queue = nc.scalar if last and q % 2 == 1 else nc.sync
+                scale_rows = y_scales[32 * q : 32 * q + 4, :]
+                queue.dma_start(out_2[g, 4 * q : 4 * q + 4, :].bitcast(I32), scale_rows.bitcast(I32))
+
+        for g in range(PASSES):
+            for t in range(PACK):
+                finish_slice(PACK * g + t)
+            store_planes(g)

@@ -87,14 +87,18 @@ def tile_list_churn_overrun_slots_kernel(
                 queue.dma_start(planes[32 * q : 32 * q + 8, :].bitcast(I32), rows.bitcast(I32))
 
         def load_scales_apart(planes, dram):
-            for q in range(QUADS):
-                rows = dram[:, 4 * q : 4 * q + 4, :].rearrange("a r c -> r a c")
-                nc.sync.dma_start(planes[32 * q : 32 * q + 4, :, :].bitcast(I32), rows.bitcast(I32))
+            rows = dram.rearrange("a (q r) c -> r q a c", r=4)
+            for r in range(4):
+                nc.sync.dma_start(planes[r:P:32, :, :].bitcast(I32), rows[r].bitcast(I32))
 
-        with nc.allow_non_contiguous_dma(reason="one value of g1 a partition and slice"):
-            nc.gpsimd.dma_start(g1_sb[:], g1.rearrange("(s p) -> p s", p=P))
-        load_scales_stacked(nc.gpsimd, w4_planes, w4_scales)
+        g1_rows = keep.tile([P, P], F32, name="g1_rows")
+        nc.gpsimd.memset(g1_rows[:], 0.0)
+        nc.gpsimd.dma_start(g1_rows[:SLICES, :], g1.rearrange("(s p) -> s p", p=P))
         make_identity(nc, ident[:])
+        load_scales_stacked(nc.gpsimd, w4_planes, w4_scales)
+        g1_bank = bank_tile("turn")
+        nc.tensor.transpose(g1_bank[:, :P], g1_rows[:], ident[:])
+        nc.scalar.copy(g1_sb[:], g1_bank[:, :SLICES])
 
         def load_list(dram, name):
             offsets = keep.tile([P, S // 16], U16, name=name)

import math
from contextlib import ExitStack

import concourse.mybir as mybir
from concourse.masks import make_identity

K, H, T, S, T2, M = 1024, 1024, 2048, 512, 2048, 512
FLOPS = 5 * 2 * K * H * S

F32 = mybir.dt.float32
BF16 = mybir.dt.bfloat16
I32 = mybir.dt.int32
U32 = mybir.dt.uint32
U16 = mybir.dt.uint16
U8 = mybir.dt.uint8
FP8X4 = mybir.dt.float8_e4m3fn_x4
FP4X4 = mybir.dt.float4_e2m1fn_x4
ALU = mybir.AluOpType
ACT = mybir.ActivationFunctionType

P = 128
PACK = 4
K_PASS = P * PACK
PASSES = K // K_PASS
QUADS = 4
SLICES = H // P
PAIRS = SLICES // 2
CHUNK = 2 * P
HALF = M // 2
LINE = 16

PAGE_CUT = T2 - T2 // 8

WIDE_BUFS = 8
RAW_BUFS = 6
STAGE_BUFS = 6
CODE_BUFS = 4
GAIN_BUFS = SLICES
H_BUFS = 6
MSET_BUFS = 5
X_BUFS = 4
BANK_BUFS = 4

TWO_PI = 2.0 * math.pi


def tile_list_churn_overrun_slots_kernel(
    tc, tab_words, tab_scales, tab2_words, tab2_scales, w1, g1, w2, w3_words, w3_scales, wg1, wg2, page0, mset,
    w4_words, w4_scales, w5, g2, offs, offs2, offs3, offs4, offs5, out_0, out_1, out_2,
):
    nc = tc.nc
    with ExitStack() as ctx:
        keep = ctx.enter_context(tc.tile_pool(name="keep", bufs=1))
        ring = ctx.enter_context(tc.tile_pool(name="ring", bufs=1))
        psum = ctx.enter_context(tc.psum_pool(name="psum", bufs=1))

        def ring_tile(tag, shape, dtype, bufs):
            return ring.tile(shape, dtype, name=tag, tag=tag, bufs=bufs, align_bytes=64)

        def wide_tile(shape, dtype):
            return ring_tile("wide", shape, dtype, WIDE_BUFS)

        def row_tile(tag, bufs, dtype=F32):
            return ring_tile(tag, [P, M], dtype, bufs)

        def stage_tile():
            return ring_tile("stage", [P, PACK * K_PASS], BF16, STAGE_BUFS)

        def bank_tile(tag):
            return psum.tile([P, M], F32, name=tag, tag=tag, bufs=BANK_BUFS)

        tab_planes = keep.tile([P, T], U8, name="tab_planes", align_bytes=64)
        tab2_planes = ring_tile("tab2_planes", [P, PASSES, T], U8, 1)
        w3_planes = keep.tile([P, PASSES, H], U8, name="w3_planes", align_bytes=64)
        w4_planes = keep.tile([P, H], U8, name="w4_planes", align_bytes=64)
        g1_sb = keep.tile([P, SLICES], F32, name="g1_sb")
        g2_sb = keep.tile([P, PASSES, PACK], F32, name="g2_sb")
        ident = keep.tile([P, P], F32, name="ident")
        nc.gpsimd.memset(tab_planes[:].bitcast(I32), 0)
        nc.vector.memset(tab2_planes[:].bitcast(I32), 0)
        nc.vector.memset(w3_planes[:].bitcast(I32), 0)
        nc.vector.memset(w4_planes[:].bitcast(I32), 0)

        def load_scales_stacked(queue, planes, dram):
            for q in range(QUADS):
                rows = dram[:, 4 * q : 4 * q + 4, :]
                queue.dma_start(planes[32 * q : 32 * q + 8, :].bitcast(I32), rows.bitcast(I32))

        def load_scales_apart(planes, dram):
            rows = dram.rearrange("a (q r) c -> r q a c", r=4)
            for r in range(4):
                nc.sync.dma_start(planes[r:P:32, :, :].bitcast(I32), rows[r].bitcast(I32))

        g1_rows = keep.tile([P, P], F32, name="g1_rows")
        nc.gpsimd.memset(g1_rows[:], 0.0)
        nc.gpsimd.dma_start(g1_rows[:SLICES, :], g1.rearrange("(s p) -> s p", p=P))
        make_identity(nc, ident[:])
        load_scales_stacked(nc.gpsimd, w4_planes, w4_scales)
        g1_bank = bank_tile("turn")
        nc.tensor.transpose(g1_bank[:, :P], g1_rows[:], ident[:])
        nc.scalar.copy(g1_sb[:], g1_bank[:, :SLICES])

        def load_list(dram, name):
            offsets = keep.tile([P, S // 16], U16, name=name)
            nc.sync.dma_start(offsets[:], dram)
            return offsets

        def gather_words(dram, a, offsets, name):
            table = wide_tile([P, T], I32)
            nc.sync.dma_start(table[:], dram[a].rearrange("p t i -> p (t i)").bitcast(I32))
            words = keep.tile([P, S], U32, name=name, align_bytes=64)
            nc.vector.tensor_copy(words[:], table[:].bitcast(U32).indirect(offsets[:]))
            return words

        def gather_scales(window, offsets, name):
            scales = keep.tile([P, S], U8, name=name, align_bytes=64)
            nc.vector.tensor_copy(scales[:], window.indirect(offsets[:]))
            return scales

        def load_piece(w, a, pair):
            raw = ring_tile("raw", [P, PACK, CHUNK], F32, RAW_BUFS)
            rows = w[a * K_PASS : (a + 1) * K_PASS, pair * CHUNK : (pair + 1) * CHUNK]
            nc.sync.dma_start(raw[:], rows.rearrange("(p j) c -> p j c", j=PACK))
            return raw

        def round_piece(stage, a, raw):
            width = CHUNK * PACK
            grouped = stage[:, a * width : (a + 1) * width].rearrange("p (c i j) -> p c j i", i=LINE // 4, j=PACK)
            nc.scalar.copy(grouped, raw[:].rearrange("p j (c i) -> p c j i", i=LINE // 4))

        def stage_chunk(w, pair):
            stage = stage_tile()
            for a in range(PASSES):
                round_piece(stage, a, load_piece(w, a, pair))
            return stage

        def quantise_chunk(stage):
            codes = ring_tile("chunk_codes", [P, PASSES * CHUNK], U32, CODE_BUFS)
            scales = ring_tile("chunk_scales", [P, PASSES * CHUNK], U8, CODE_BUFS)
            nc.vector.quantize_mx(out=codes[:].bitcast(FP8X4), scales=scales[:], in_=stage[:])
            return codes, scales

        def chunk_cols(a, s):
            first = a * CHUNK + (s % 2) * P
            return slice(first, first + P)

        pages, h1, gains, h2, x_rows = {}, {}, {}, {}, {}

        def load_page(s, cols):
            if s not in pages:
                pages[s] = wide_tile([P, T2], F32)
            nc.sync.dma_start(pages[s][:, cols], page0[s * P : (s + 1) * P, cols])

        def make_h1(s):
            codes, scales = w1_chunks[s // 2]
            acc = bank_tile("product")
            for a in range(PASSES):
                cols = chunk_cols(a, s)
                nc.tensor.matmul_mx(
                    out=acc[:], lhsT=codes[:, cols].bitcast(FP8X4), lhsT_scale=scales[:, cols],
                    rhs=v_words[a][:].bitcast(FP8X4), rhs_scale=v_scales[4 * a : P, :],
                    start=(a == 0), stop=(a == PASSES - 1),
                )
            gains[s] = row_tile("gain", GAIN_BUFS)
            nc.scalar.activation(gains[s][:], wg1_sb[:], ACT.Copy, scale=g1_sb[:, s : s + 1])
            h1[s] = row_tile("h", H_BUFS)
            nc.scalar.activation(h1[s][:], acc[:], ACT.Tanh)

        def put_h1(s):
            nc.vector.tensor_tensor(pages[s][:].indirect(list3[:]), h1[s][:], gains[s][:], ALU.mult)

        def make_h2(s):
            codes, scales = w2_chunks[s // 2]
            acc = bank_tile("product")
            for a in range(PASSES):
                cols = chunk_cols(a, s)
                nc.tensor.matmul_mx(
                    out=acc[:], lhsT=codes[:, cols].bitcast(FP8X4), lhsT_scale=scales[:, cols],
                    rhs=v2_words[a][:].bitcast(FP8X4), rhs_scale=v2_scales[a][:],
                    start=(a == 0), stop=False,
                )
            for a in range(PASSES):
                nc.tensor.matmul_mx(
                    out=acc[:], lhsT=w3_sb[:, a, 2 * s * P : 2 * (s + 1) * P].bitcast(FP4X4),
                    lhsT_scale=w3_planes[:, a, s * P : (s + 1) * P],
                    rhs=v2_words[a][:].bitcast(FP8X4), rhs_scale=v2_scales[a][:],
                    start=False, stop=(a == PASSES - 1),
                )
            h2[s] = row_tile("h_last", 1) if s == SLICES - 1 else row_tile("h", H_BUFS)
            nc.scalar.copy(h2[s][:], acc[:])

        def put_h2(s):
            nc.vector.tensor_tensor(pages[s][:].indirect(list4[:]), h2[s][:], wg2_sb[:], ALU.mult)

        def read_page(s):
            x_rows[s] = row_tile("x", X_BUFS)
            nc.vector.tensor_copy(x_rows[s][:], pages[s][:].indirect(list5[:]))
            nc.gpsimd.dma_start(out_0[s * P : (s + 1) * P, :], x_rows[s][:])

        x_dealt = {}

        def deal_x(g):
            x_dealt[g] = wide_tile([P, PACK, M], F32)
            rows = out_0[g * K_PASS : (g + 1) * K_PASS, :]
            nc.sync.dma_start(x_dealt[g][:], rows.rearrange("(p t) m -> p t m", t=PACK))

        z_turned = [
            keep.tile([P, M // P, 2, P, 2], BF16, name="z_turned%d" % a, align_bytes=64) for a in range(PASSES)
        ]
        z_stage, z_codes, z_scales = {}, {}, {}

        def add_mset(s):
            mset_rows = row_tile("mset", MSET_BUFS)
            nc.sync.dma_start(mset_rows[:], mset[s * P : (s + 1) * P, :])
            bank = bank_tile("turn")
            blocks = [(term, c) for term in (mset_rows, x_rows[s]) for c in range(M // P)]
            for i, (term, c) in enumerate(blocks):
                nc.tensor.matmul(
                    bank[:, c * P : (c + 1) * P], term[:, c * P : (c + 1) * P], ident[:],
                    start=(i == 0), stop=(i == len(blocks) - 1), is_transpose=True,
                )
            a, q = divmod(s, QUADS)
            nc.scalar.copy(
                z_turned[a][:, :, :, 32 * q : 32 * q + 32, :],
                bank[:].rearrange("i (c p u e) -> i c u p e", c=M // P, u=2, e=2),
            )

        def turn_z(a):
            words = z_turned[a][:].rearrange("i c u p e -> i (c u p e)").bitcast(F32)
            z_stage[a] = stage_tile()
            stage_words = z_stage[a][:].bitcast(F32)
            for half in range(2):
                bank = bank_tile("turn")
                for c in range(2):
                    for u in range(2):
                        source = ((2 * half + c) * 2 + u) * P
                        target = u * HALF + c * P
                        nc.tensor.transpose(bank[:, target : target + P], words[:, source : source + P], ident[:])
                nc.scalar.copy(
                    stage_words[:, half * M : (half + 1) * M].rearrange("p (m u) -> p m u", u=2),
                    bank[:].rearrange("p (u m) -> p m u", u=2),
                )

        def quantise_z(a, codes):
            z_codes[a] = codes
            z_scales[a] = keep.tile([P, M], U8, name="z_scales%d" % a, align_bytes=64)
            nc.vector.quantize_mx(out=codes.bitcast(FP8X4), scales=z_scales[a][:], in_=z_stage[a][:])

        w5_stage, w4_raw = {}, {}

        def stage_w5(a, g):
            w5_stage[(a, g)] = stage_tile()
            grouped = w5_stage[(a, g)][:].rearrange("p (t m j) -> p m j t", t=PACK, j=PACK)
            raw = wide_tile([P, PACK, K_PASS], F32)
            rows = w5[a * K_PASS : (a + 1) * K_PASS, g * K_PASS : (g + 1) * K_PASS]
            nc.sync.dma_start(raw[:], rows.rearrange("(p j) c -> p j c", j=PACK))
            loaded = raw[:].rearrange("p j (m t) -> p m j t", t=PACK)
            for part in (slice(0, P // 2), slice(P // 2, P)):
                nc.scalar.copy(grouped[:, part, :, :], loaded[:, part, :, :])

        def load_w4(g):
            w4_raw[g] = keep.tile([P, PASSES, K_PASS], I32, name="w4_raw%d" % g, align_bytes=64)
            words = w4_words[:, :, g * K_PASS : (g + 1) * K_PASS, :].rearrange("a p c i -> p a (c i)")
            nc.sync.dma_start(w4_raw[g][:], words.bitcast(I32))

        whole = slice(0, T2)
        first_piece = load_piece(w1, 0, 0)
        list1 = load_list(offs, "list1")
        load_scales_stacked(nc.sync, tab_planes, tab_scales)
        second_piece = load_piece(w1, 1, 0)
        first_stage = stage_tile()
        round_piece(first_stage, 0, first_piece)
        round_piece(first_stage, 1, second_piece)
        w1_chunks = {0: quantise_chunk(first_stage)}
        wg1_sb = keep.tile([P, S], F32, name="wg1_sb")
        v_scales = gather_scales(tab_planes[:], list1, "v_scales")
        v_words = [gather_words(tab_words, a, list1, "v_words%d" % a) for a in range(PASSES)]
        nc.sync.dma_start(wg1_sb[:], wg1)
        list3 = load_list(offs3, "list3")
        load_page(0, whole)
        make_h1(0)
        make_h1(1)
        put_h1(0)

        load_scales_apart(tab2_planes, tab2_scales)
        list2 = load_list(offs2, "list2")
        v2_scales = [gather_scales(tab2_planes[:, a, :], list2, "v2_scales%d" % a) for a in range(PASSES)]
        v2_words = {0: gather_words(tab2_words, 0, list2, "v2_words0")}
        w2_chunks = {0: quantise_chunk(stage_chunk(w2, 0))}
        v2_words[1] = gather_words(tab2_words, 1, list2, "v2_words1")
        load_page(1, whole)
        put_h1(1)
        load_scales_apart(w3_planes, w3_scales)
        w3_sb = keep.tile([P, PASSES, 2 * H], U8, name="w3_sb", align_bytes=64)
        nc.sync.dma_start(w3_sb[:].bitcast(I32), w3_words.rearrange("a p c -> p a c").bitcast(I32))
        wg2_sb = ring_tile("wg2", [P, S], F32, 1)
        nc.sync.dma_start(wg2_sb[:], wg2)
        list4 = load_list(offs4, "list4")
        make_h2(0)
        make_h2(1)
        put_h2(0)
        put_h2(1)
        w1_chunks[1] = quantise_chunk(stage_chunk(w1, 1))
        w2_chunks[1] = quantise_chunk(stage_chunk(w2, 1))
        list5 = load_list(offs5, "list5")
        read_page(0)
        read_page(1)

        w5_blocks = [(a, g) for g in range(PASSES) for a in range(PASSES)]
        for pair in range(1, PAIRS):
            slices = (2 * pair, 2 * pair + 1)
            more = pair + 1 < PAIRS
            for make in (make_h1, make_h2):
                for s in slices:
                    make(s)
            if pair == PAIRS - 2:
                stage_w5(*w5_blocks[0])
                for s in range(QUADS):
                    add_mset(s)
                turn_z(0)
            if pair == PAIRS - 1:
                for block in w5_blocks[1:]:
                    stage_w5(*block)
                for s in range(QUADS, 2 * pair):
                    add_mset(s)
            for s in slices:
                load_page(s, slice(0, PAGE_CUT))
            if more:
                next_stage = stage_chunk(w1, pair + 1)
            for s in slices:
                load_page(s, slice(PAGE_CUT, T2))
            for put in (put_h1, put_h2):
                for s in slices:
                    put(s)
            if more:
                w1_chunks[pair + 1] = quantise_chunk(next_stage)
            for s in slices:
                read_page(s)
            if more:
                w2_chunks[pair + 1] = quantise_chunk(stage_chunk(w2, pair + 1))
        add_mset(SLICES - 2)
        add_mset(SLICES - 1)
        turn_z(1)

        late_codes = ring_tile("h_last", [P, PASSES * H + M], U32, 1)
        quantise_z(1, row_tile("z_codes", 1, U32)[:])
        quantise_z(0, late_codes[:, PASSES * H :])
        load_w4(0)
        load_w4(1)
        nc.sync.dma_start(g2_sb[:], g2.rearrange("(g p t) -> p g t", p=P, t=PACK))
        deal_x(0)
        deal_x(1)

        w4_codes = ring_tile("wg2", [P, PASSES, H], I32, 1)
        w4_dealt_planes = ring_tile("tab2_planes", [P, H], U8, 1)
        w5_codes = late_codes[:, : PASSES * H].rearrange("p (a c) -> p a c", a=PASSES)
        w5_planes = keep.tile([P, PASSES, H], U8, name="w5_planes", align_bytes=64)
        nc.vector.tensor_copy(
            w4_dealt_planes[:].rearrange("p (g t b i) -> p g b t i", g=PASSES, t=PACK, i=LINE),
            w4_planes[:].rearrange("p (g b i t) -> p g b t i", g=PASSES, t=PACK, i=LINE),
        )
        for g in range(PASSES):
            group = slice(g * K_PASS, (g + 1) * K_PASS)
            nc.vector.tensor_copy(
                w4_codes[:, :, group].rearrange("p a (t b i) -> p a b t i", t=PACK, i=LINE // 4),
                w4_raw[g][:].rearrange("p a (b i t) -> p a b t i", t=PACK, i=LINE // 4),
            )
            for a in range(PASSES):
                nc.vector.quantize_mx(
                    out=w5_codes[:, a, group].bitcast(FP8X4), scales=w5_planes[:, a, group], in_=w5_stage[(a, g)][:]
                )

        out_rows = out_0.rearrange("(g p t) m -> g t p m", p=P, t=PACK)
        y_rows = {}

        def second_product(n, codes, planes):
            cols = slice(n * P, (n + 1) * P)
            in_turn_bank = n % 4 >= 2
            bank = bank_tile("turn" if in_turn_bank else "product")
            for i, a in enumerate((1, 0) if in_turn_bank else (0, 1)):
                nc.tensor.matmul_mx(
                    out=bank[:], lhsT=codes[:, a, cols].bitcast(FP8X4), lhsT_scale=planes[a][:, cols],
                    rhs=z_codes[a].bitcast(FP8X4), rhs_scale=z_scales[a][:], start=(i == 0), stop=(i == 1),
                )
            return bank

        def finish_slice(n):
            g, t = divmod(n, PACK)
            if t == 0:
                y_rows[g] = wide_tile([P, PACK, M], F32)
            angle = second_product(n, w4_codes, [w4_dealt_planes[4 * a : P, :] for a in range(PASSES)])
            lin = second_product(n, w5_codes, [w5_planes[:, a, :] for a in range(PASSES)])

            turns = row_tile("gain", GAIN_BUFS, I32)
            nc.vector.tensor_scalar(turns[:], angle[:], 1.0 / TWO_PI, 0.25, ALU.mult, ALU.add)
            factor = row_tile("h", H_BUFS)
            nc.vector.scalar_tensor_tensor(
                factor[:], x_dealt[g][:, t, :], g2_sb[:, g, t : t + 1], lin[:], ALU.mult, ALU.add
            )
            reduced = row_tile("mset", MSET_BUFS)
            cosine = row_tile("x", X_BUFS)
            last = n == SLICES - 1
            engine = nc.vector if last else nc.gpsimd
            parts = (slice(0, HALF), slice(HALF, M)) if last else (slice(0, M),)
            for part in parts:
                nc.vector.scalar_tensor_tensor(
                    reduced[:, part], turns[:, part], -TWO_PI, angle[:, part], ALU.mult, ALU.add
                )
                nc.scalar.activation(cosine[:, part], reduced[:, part], ACT.Sin, bias=math.pi / 2)
            for part in parts:
                engine.tensor_tensor(y_rows[g][:, t, part], cosine[:, part], factor[:, part], ALU.mult)
            nc.sync.dma_start(out_rows[g, t], y_rows[g][:, t, :])

        def store_planes(g):
            last = g == PASSES - 1
            stage = stage_tile()
            y_codes = keep.tile([P, M], U32, name="y_codes%d" % g, align_bytes=64)
            y_scales = keep.tile([P, M], U8, name="y_scales%d" % g, align_bytes=64)
            words_out = out_1[g].rearrange("p m t -> p (m t)").bitcast(I32)
            for half in range(2):
                part = slice(half * HALF, (half + 1) * HALF)
                staged = stage[:, half * HALF * PACK : (half + 1) * HALF * PACK]
                grouped = staged.rearrange("p (c i t) -> p c t i", i=LINE // 4, t=PACK)
                rows = y_rows[g][:, :, part].rearrange("p t (c i) -> p c t i", i=LINE // 4)
                if last and half == 1:
                    nc.vector.tensor_copy(grouped, rows)
                else:
                    nc.scalar.copy(grouped, rows)
                nc.vector.quantize_mx(out=y_codes[:, part].bitcast(FP8X4), scales=y_scales[:, part], in_=staged)
                nc.sync.dma_start(words_out[:, part], y_codes[:, part].bitcast(I32))
            for q in range(QUADS):
                queue = nc.scalar if last and q % 2 == 1 else nc.sync
                scale_rows = y_scales[32 * q : 32 * q + 4, :]
                queue.dma_start(out_2[g, 4 * q : 4 * q + 4, :].bitcast(I32), scale_rows.bitcast(I32))

        for g in range(PASSES):
            for t in range(PACK):
                finish_slice(PACK * g + t)
            store_planes(g)
